import numpy as np, ml_dtypes
CORES = [16,17,18,19,32,33,34,35]
N = 8
BF = ml_dtypes.bfloat16
P, TW, M, RO = 2048, 4096, 4, 5
def parts(rng):
    v = rng.integers(0, 128, (N, 8, 16, P)); v[:, :, 15] = rng.integers(0, 2, (N, 8, P))
    t = rng.integers(0, 128, (N, 8, 16, TW)); t[:, :, 15] = rng.integers(0, 2, (N, 8, TW))
    return v, t, rng.integers(1, 256, (N, 8, 16)), rng.integers(0, 2048, (N, 8, RO, M))
def pack(v, t, w, k):
    return {"x": v.reshape(N, 128, P).astype(np.float32).astype(BF), "tm": t.reshape(N, 128, TW).astype(np.float32).astype(BF),
            "wt": np.ascontiguousarray(w.reshape(N, 128, 1)).astype(np.int32),
            "km": np.repeat(k.reshape(N, 8, 1, RO * M), 16, axis=2).reshape(N, 128, RO * M).astype(np.int32)}
def aim(rng, q, noth):
    u = np.arange(1, 4096, 2); i = u.copy()
    for _ in range(4): i = (i * (2 - u * i)) & 4095
    kk = ((q - (u * u >> 5)) * i) & (P - 1)
    ok = np.flatnonzero((kk < 2048) & (((u * u >> 4) & (TW - 1)) != noth))
    s = int(rng.choice(ok)); return int(u[s]), int(kk[s])
def column(rng, w, u, s):
    c = rng.integers(0, 128, 16); c[15] = s; c[:2] = 0
    z = (u - int(np.sum(w * c))) & 4095; c[0] = z & 63; c[1] = z >> 6
    return c
def setup_inputs(rng):
    return pack(*parts(rng))
def setup_inputs_ends(rng):
    v, t, w, k = parts(rng); w[:, :, 0] = 1; w[:, :, 1] = 64; w[:, :, 15] = 0
    for r in range(N):
        o = (r + 1) % N
        for g in range(8):
            case = (g - r) % 9
            a = int(rng.integers(1, P // 4)); b = int(rng.integers(P // 2, 3 * P // 4))
            if case < 2: a, b = 0, P - 1
            if case in (2, 3): b = a + 1
            if case == 8: a, b = int(rng.integers(1, P // 8)), int(rng.integers(7 * P // 8, P - 8))
            p, q = a, b
            if case == 7 or (case < 6 and rng.random() < 0.5): p, q = b, a
            s = int(rng.integers(0, 2)); u, k[r, g, 0, 0] = aim(rng, q, -1); c = column(rng, w[r, g], u, s); h = (u * u >> 4) & (TW - 1)
            if case == 4: v[r, g, 15] = s
            v[r, g, :, p] = c; v[r, g, :, q] = c
            if case in (0, 3): v[r, g, 15, q] = 1 - s
            t[o, g, :15, h] = c[:15]
            if case == 6: v[r, g, :, int(rng.integers(a + 1, b))] = c
            if case == 7: v[r, g, :, b + 3] = c
            if case in (1, 4, 5, 7, 8):
                p2, q2 = {1: (P // 3, P // 2), 4: (a + 1, P - 1), 5: (b - 1, b + 1), 7: (a + 2, b - 2), 8: (P // 2, P - 3)}[case]
                if (case == 4 and r % 2 == 0) or rng.random() < 0.5: p2, q2 = q2, p2
                u2, k[r, g, 0, 1] = aim(rng, q2, h); c2 = column(rng, w[r, g], u2, s if case == 4 else int(rng.integers(0, 2))); h2 = (u2 * u2 >> 4) & (TW - 1)
                v[r, g, :, p2] = c2; v[r, g, :, q2] = c2; t[o, g, :15, h2] = c2[:15]; t[o, g, 0, h2] = c2[0] ^ (2 if case == 8 else 1)
            if case == 8:
                ks = np.arange(2048); zs = ((u * u >> 5) + ks * u) & (P - 1)
                ks = ks[(zs > a) & (zs < b) & (zs != P // 2)]
                k[r, g, 0, 2] = int(rng.choice(ks)); z = ((u * u >> 5) + int(k[r, g, 0, 2]) * u) & (P - 1)
                cz = c.copy(); cz[0] = c[0] ^ 1; uz = (u + int(cz[0]) - int(c[0])) & 4095
                v[r, g, :, z] = cz; t[o, g, :15, (u * uz >> 4) & (TW - 1)] = c[:15]
    return pack(v, t, w, k)
def setup_inputs_kinds(rng):
    v, t, w, k = parts(rng); w[:] = w[:1].copy(); w[:, :, 15] = 0
    for g in (0, 2, 4):
        w[:, g, 0] = 1; w[:, g, 1] = 64; w[:, g, (2 if g == 2 else 8):] = 0
        u = 3 if g == 4 else 2 * int(rng.integers(0, 2048)) + 1; c = column(rng, w[0, g], u, 0)
        if g != 2: v[:, g, :8] = c[:8, None]
        else:
            v[:, g, :2] = c[:2, None]; v[:, g, 2:15] = rng.integers(0, 41, (N, 13, P)); k[:, g, 0] = k[:, g, 0, :1].copy()
            for r in range(N): v[r, g, 2:15, ((u * u >> 5) + int(k[r, g, 0, 0]) * u) & (P - 1)] = rng.integers(120, 128, 13)
    for g in (1, 3, 5, 6, 7):
        n = 5 if g % 2 else int(rng.integers(2, 6)); kd = rng.integers(0, 128, (16, n))
        if g % 2:
            kd[:, 4] = rng.integers(40, 88, 16)
            kd[:, :4] = kd[:, 4:] + rng.integers(8, 41, (16, 4)) * (2 * rng.integers(0, 2, (16, 4)) - 1)
        for r in range(N):
            kind = rng.integers(0, n, P)
            if g % 2:
                c = r % 4; uc, u4 = [int(np.sum(w[r, g] * kd[:, i])) & 4095 for i in (c, 4)]
                kind[((u4 * u4 >> 5) + k[r, g, 0] * u4) & (P - 1)] = c
                t[(r + 1) % N, g, :15, (uc * u4 >> 4) & (TW - 1)] = (kd[:15, c] + kd[:15, 4]) >> 1
            v[r, g] = kd[:, kind]
    v[:, :, 15] = rng.integers(0, 2, (N, 8, P))
    return pack(v, t, w, k)
def setup_inputs_void(rng):
    v, t, w, k = parts(rng); w[:, :, 0] = 1; w[:, :, 1] = 64; k[:, ::2] = k[:, ::2, :1, :1].copy()
    for g in (0, 6):
        v[:, g, 2:15] &= 3; t[:, g, :15] = 124 + (t[:, g, :15] & 3)
    us = np.arange(4096); j = np.arange(P)
    for r in range(N):
        for g in range(8):
            pre = np.full(P, -1); pre[((us * us >> 5) + int(k[r, g, 0, 0]) * us) & (P - 1)] = us
            z = (pre - np.sum(w[r, g, 2:, None] * v[r, g, 2:], axis=0)) & 4095
            v[r, g, 0] = np.where(pre >= 0, z & 63, v[r, g, 0]); v[r, g, 1] = np.where(pre >= 0, z >> 6, v[r, g, 1])
            if g in (0, 6):
                u = np.sum(w[r, g, :, None] * v[r, g], axis=0) & 4095; q = ((u * u >> 5) + int(k[r, g, 0, 0]) * u) & (P - 1)
                h = (u * u[q] >> 4) & (TW - 1); free = np.flatnonzero((q == j) & ~np.isin(h, h[q != j]))
                if len(free):
                    p = int(rng.choice(free)); t[(r + 1) % N, g, :15, int(h[p])] = v[r, g, :15, p]
    return pack(v, t, w, k)
def setup_inputs_small(rng):
    v, t, w, k = parts(rng)
    return pack(v & 1, t & 1, w, k)
def setup_inputs_spread(rng):
    v, t, w, k = parts(rng); both = []
    for a in (v, t):
        n = a.shape[-1]; b = np.minimum((np.exp2(8 * rng.random((N, 8, 1, n))) * rng.random(a.shape)).astype(np.int64), 127)
        z = rng.integers(0, 32, (N, 8, 1, n)); b = np.where(z == 0, 0, np.where(z == 1, 127, b)); b[:, :, 15] = a[:, :, 15]; both.append(b)
    w = np.minimum(np.exp2(8.1 * rng.random((N, 8, 16))).astype(np.int64), 255); w[:, :, 3] = 0; w[:, :, 4] = 255
    w[:, 5] = rng.integers(200, 256, (N, 16)); w[:, 6] = 255
    both[0][:, 5, :15] = rng.integers(100, 128, (N, 15, P)); both[0][:, 6, :15] = rng.integers(64, 128, (N, 15, P))
    both[0][:, 6, :15, P - 1] = 127; both[0][:, 6, 15, P - 1] = 1
    k = np.minimum(np.exp2(11.1 * rng.random((N, 8, RO, M))).astype(np.int64) - 1, 2047); k[:, 1, 0, 0] = 0; k[:, 2, 0, 1] = 2047
    return pack(both[0], both[1], w, k)
def check_inputs(d):
    bad = []
    for name in ("x", "tm"):
        a = np.asarray(d[name]).astype(np.float32)
        if not np.all((a >= 0) & (a <= 127) & (np.floor(a) == a)): bad.append("whole numbers of " + name)
        if not np.all(a[:, 15::16] <= 1): bad.append("signs of " + name)
    for name, hi in (("wt", 255), ("km", 2047)):
        if np.min(d[name]) < 0 or np.max(d[name]) > hi: bad.append("range of " + name)
    a = np.asarray(d["km"]); a = a.reshape(a.shape[0], 8, 16, -1)
    if not np.all(a == a[:, :, :1]): bad.append("rows of km alike")
    return bad
def reference(x, tm, wt, km):
    v = x.astype(np.float32).astype(np.int32).reshape(N, 8, 16, P); tp = tm.astype(np.float32).astype(np.int32).reshape(N, 8, 16, TW)
    w = wt.astype(np.int32).reshape(N, 8, 16, 1); k = km.astype(np.int32).reshape(N, 8, 16, RO, M)[:, :, 0]; j = np.arange(P)
    for t in range(RO):
        u = np.add.reduce(w * v, axis=2, dtype=np.int32) & 4095
        bq = bd = None
        for m in range(M):
            q = ((u * u >> 5) + k[:, :, t, m][:, :, None] * u) & (P - 1)
            xq = np.take_along_axis(v, q[:, :, None, :], 3)
            dm = np.where(q == j, 8192, np.add.reduce(np.abs(v - xq)[:, :, :15], axis=2))
            if m == 0: bq, bd = q, dm
            else: bq, bd = np.where(dm < bd, q, bq), np.minimum(bd, dm)
        xq = np.take_along_axis(v, bq[:, :, None, :], 3)
        h = (u * np.take_along_axis(u, bq, 2) >> 4) & (TW - 1)
        got = np.stack([np.take_along_axis(tp[(r + 1 + t % (N - 1)) % N], h[r][:, None, :], 2) for r in range(N)])
        e = bd + np.add.reduce(np.abs(v + xq - 2 * got)[:, :, :15], axis=2)
        alike = v[:, :, 15] == xq[:, :, 15]; lo = np.minimum(j, bq); hi = np.maximum(j, bq)
        nv = np.empty_like(v)
        for r in range(N):
            for g in range(8):
                p = int(np.argmin(e[r, g])); a, b = int(lo[r, g, p]), int(hi[r, g, p])
                z = v[r, g].copy(); z[:15, a] = (v[r, g, :15, a] + v[r, g, :15, b]) >> 1
                tp[r, g, :, int(h[r, g, p])] = z[:, a]
                if not alike[r, g, p]:
                    z[:, a + 1:b + 1] = z[:, a + 1:b + 1][:, ::-1].copy(); z[15, a + 1:b + 1] = 1 - z[15, a + 1:b + 1]
                else:
                    c, d = b, P - 1
                    inside = alike[r, g] & (lo[r, g] > a) & (lo[r, g] < b)
                    if np.any(inside):
                        p2 = int(np.argmin(np.where(inside, e[r, g], 2 ** 20)))
                        if hi[r, g, p2] > b: c, d = int(lo[r, g, p2]), int(hi[r, g, p2])
                    z = z[:, np.concatenate([j[:a + 1], j[b + 1:d + 1], j[c + 1:b + 1], j[a + 1:c + 1], j[d + 1:]])]
                nv[r, g] = z
        v = nv
    return {"y": v.reshape(N, 128, P).astype(np.float32).astype(BF)}

@@ -1,0 +1,575 @@
+from concourse.mybir import AluOpType as A, AxisListType as AX, ActivationFunctionType as F
+
+RO, M, P, TW = 5, 4, 2048, 4096
+W0 = 16
+NX = W0 + 2 * P
+N0 = 56
+PART = ((0, N0), (N0, 128))
+VIT = {(0, 0), (0, 1), (1, 0), (1, 1), (3, 0)}
+PORD = (1, 0)
+MORD = (2, 0, 3, 1)
+NPV = 64
+BX, BP = 3.0, 1.0
+
+SCRATCH = {}
+_PS = ["p%d" % i for i in range(8)]
+_B2 = ("bfloat16", "float16", "uint16")
+_CS = {n: i for i, n in enumerate("kg15 kg kr k odd r15 fm half dbl flw wf wu w1 mk0 padc dvc dsc bec f2 mone r1 kmin ar har hpf nf kmin2 "
+                                  "a b dir inv ba aC aI bI m1 m3 x3 K2 cdef ddef xd an1 xC xI c d f valid xc xe ce de t2 t3 m2 m4".split())}
+_CI = {n: i for i, n in enumerate("ik ikg ikr iodd ni".split())}
+for _a in _PS:
+    SCRATCH[_a] = ("psum", [128, 512], "float32")
+for _d, _l in (("bfloat16", (("xin", P), ("tmo", TW), ("xb0", NX), ("xb1", NX), ("yo", P), ("xc", P), ("mb", 144), ("bu", 144), ("bf", 144), ("bs", 144), ("bds", 144), ("be", 144),
+                             ("ib", 128), ("nib", 128), ("d2kb", 128), ("dvoid", 128), ("lx", 128), ("cm", 384), ("eq", 512), ("gm", 4 * P), ("ab", 4 * P), ("vc", 128),
+                             ("dir", 128), ("sp", P), ("gq", P), ("rr", P), ("ga", P), ("ab2", P), ("t1", 128), ("t2", 128)) + tuple(("tb%d" % k, TW + 16) for k in range(RO))),
+               ("float16", (("bdv", 144), ("i16", 128), ("ni16", 128), ("p2i", 128), ("m2i", 128), ("d2k16", 128), ("dn8k", 128), ("pw16", 128), ("f1", 128), ("q16", 512),
+                            ("mx", 4 * P), ("d16", 128), ("qs16", 128), ("cc", 128), ("gt", 896))),
+               ("float32", (("xw", P), ("cs", 64), ("kmf", RO * M), ("lxa", 128), ("lxc", 128), ("ob", 128), ("mk16", 16), ("pwf", 128), ("b0", 128), ("b1", 128), ("b2", 128),
+                            ("cmn", 128), ("dg", 16), ("oh", 128), ("pr", 128), ("hpr", 128), ("k2a", 128), ("k2", 128), ("oh2", 128), ("nc", 16), ("upv", 16))),
+               ("int32", (("wti", 1), ("kmi", RO * M), ("ci", 8), ("ij", 144), ("ic", 128), ("jb", 128), ("ui", 128), ("u", 128), ("sq", 128), ("sh", 128), ("qv", 512), ("qi", 512),
+                          ("bk", 128), ("q", 128), ("di", 128), ("uq", 128), ("uq2", 128), ("uu", 128), ("h", 128), ("ka", 2), ("pq", 2), ("kb", 2), ("pb", 2))),
+               ("uint16", (("ql", 512), ("qsl", 128), ("hl", 128), ("nl", 2), ("pl", 128), ("msg", 128), ("land", 320)))):
+    for _a, _c in _l:
+        SCRATCH[_a] = ("sbuf", [128, _c], _d)
+_LK = [(t, s) for t in range(1, RO) for s in range(t)]
+SEMAPHORES = (["sv", "ss", "st", "sg", "lmsg", "lown", "lx0", "lx1", "lw", "lk", "lt0", "lt1", "lt2", "lt3", "st0", "st1"] + ["xc%d" % k for k in range(RO)]
+              + ["ta%d" % k for k in range(RO)] + ["ls%d" % k for k in range(4)] + ["m%d_%d" % ts for ts in _LK])
+
+CYC, TCY, GC, WAKE, SELF = 0.83e-3 * 1.25, 0.42e-3 * 1.25, 1.56, 0.15, 0.06
+
+
+def _ap(T, r):
+    return T[r[0]][:, r[1]:r[2]] if len(r) == 3 else T[r[0]][:, r[1]:r[2]:r[3]]
+
+
+def _n(r):
+    return r[2] - r[1]
+
+
+def _ps(r):
+    return r[0] in _PS
+
+
+def C(n):
+    return ("cs", _CS[n], _CS[n] + 1) if n in _CS else ("ci", _CI[n], _CI[n] + 1)
+
+
+def build():
+    ops, BST, AFT = [], [0.0], []
+
+    def add(q, cost, emit, reads, writes, done=None, after=()):
+        ops.append({"q": q, "cost": cost, "emit": emit, "reads": reads, "writes": writes, "done": done, "after": list(after) + AFT, "boost": BST[0]})
+        return len(ops) - 1
+
+    def isc(*xs):
+        return [x for x in xs if isinstance(x, tuple)]
+
+    def val(T, x):
+        return _ap(T, x) if isinstance(x, tuple) else x
+
+    def fast(*rs):
+        return 0.5 if all((not _ps(r)) and SCRATCH[r[0]][2] in _B2 for r in rs) else 1.0
+
+    def vt(out, a, b, op):
+        c = _n(out) * (1 if _ps(a) or _ps(b) else 2)
+        add("v", max(64, c) * CYC, lambda g, T, x: g.vector.tensor_tensor(_ap(T, out), _ap(T, a), _ap(T, b), op), [a, b], [out])
+
+    def vs(out, a, s1, op0, s2=None, op1=None):
+        def e(g, T, x):
+            if op1 is None:
+                return g.vector.tensor_scalar(_ap(T, out), _ap(T, a), val(T, s1), None, op0)
+            return g.vector.tensor_scalar(_ap(T, out), _ap(T, a), val(T, s1), val(T, s2), op0, op1)
+        return add("v", max(64, _n(out) * fast(out, a)) * CYC, e, [a] + isc(s1, s2), [out])
+
+    def vcopy(out, a):
+        add("v", max(64, _n(out) * fast(out, a)) * CYC, lambda g, T, x: g.vector.tensor_copy(_ap(T, out), _ap(T, a)), [a], [out])
+
+    def vred(out, a, op):
+        add("v", max(64, _n(a)) * CYC, lambda g, T, x: g.vector.tensor_reduce(_ap(T, out), _ap(T, a), AX.X, op), [a], [out])
+
+    def vset(out, c):
+        add("v", max(64, _n(out)) * CYC, lambda g, T, x: g.vector.memset(_ap(T, out), c), [], [out])
+
+    def vgt(out, win, off, b, op):
+        add("v", 0.05 + _n(out) * GC * CYC, lambda g, T, x: g.vector.tensor_tensor(_ap(T, out), _ap(T, win).indirect(_ap(T, off)), _ap(T, b), op), [win, off, b], [out])
+
+    def vgs(out, win, off, s):
+        add("v", 0.05 + _n(out) * GC * CYC, lambda g, T, x: g.vector.tensor_scalar(_ap(T, out), _ap(T, win).indirect(_ap(T, off)), val(T, s), None, A.mult), [win, off] + isc(s), [out])
+
+    def sa(out, a, func, bias=0.0, scale=1.0):
+        return add("s", (60 + max(64, _n(out))) * CYC, lambda g, T, x: g.scalar.activation(_ap(T, out), _ap(T, a), func, bias=val(T, bias), scale=val(T, scale)), [a] + isc(bias, scale), [out])
+
+    def lin(out, a, scale, bias):
+        sa(C(out), C(a), F.Identity, bias=bias, scale=scale)
+
+    def sg(out, win, off, bias=0.0, scale=1.0):
+        add("s", 0.065 + _n(out) * GC * CYC, lambda g, T, x: g.scalar.activation(_ap(T, out), _ap(T, win).indirect(_ap(T, off)), F.Identity, bias=bias, scale=val(T, scale)), [win, off] + isc(scale), [out])
+
+    def mm(out, parts, start=True, stop=True):
+        cost = len(parts) * max(64, _n(out)) * TCY * (4 if SCRATCH[parts[0][0][0]][2] == "float32" else 1)
+
+        def e(g, T, x):
+            for k, (l, r) in enumerate(parts):
+                i = g.tensor.matmul(_ap(T, out), _ap(T, l), _ap(T, r), start and k == 0, stop and k == len(parts) - 1)
+            return i
+        add("t", cost, e, [y for lr in parts for y in lr] + ([] if start else [out]), [out])
+
+    def wrapped(b, src, c0, n):
+        return [((b, 15 - i, 143 - i), (src, c0 + i, c0 + n, 16)) for i in range(16)]
+
+    def ld(sem, q, out, src, c0, c1):
+        add(q, 0.1, lambda g, T, x: (g.sync if q == "d" else g.scalar).dma_start(_ap(T, out), T[src][:, c0:c1]), [], [out], done=lambda x: (sem, 16))
+
+    def blocks(n):
+        return [(b, min(b + 512, n)) for b in range(0, n, 512)]
+
+    ld("lx0", "d", ("xin", 0, 1024), "x", 0, 1024)
+    ld("lx1", "sd", ("xin", 1024, P), "x", 1024, P)
+    ld("lw", "d", ("wti", 0, 1), "wt", 0, 1)
+    ld("lk", "d", ("kmi", 0, RO * M), "km", 0, RO * M)
+    for k in range(4):
+        ld("lt%d" % k, "d" if k % 2 else "sd", ("tmo", k * 1024, k * 1024 + 1024), "tm", k * 1024, k * 1024 + 1024)
+
+    def iota(out, pat, base, cmul):
+        add("g", 0.3, lambda g, T, x: g.iota(_ap(T, out), pat, base, cmul), [], [out])
+
+    def full(n, c=128):
+        return (n, 0, c)
+    iota(C("ik"), [[1, 1]], 0, 1)
+    iota(full("ij", 144), [[1, 144]], 0, 0)
+    iota(full("ic"), [[16, 128]], 0, 0)
+    ij, J, mb, PWP = full("ij"), full("ij", 144), full("mb", 144), ("p0", 256, 384)
+    vs(C("ikg"), C("ik"), 112, A.bitwise_and)
+    vs(C("ikr"), C("ik"), 15, A.bitwise_and)
+    vcopy(C("k"), C("ik"))
+    vcopy(C("kr"), C("ikr"))
+    vs(C("kg15"), C("ikg"), 15.0, A.add)
+    vs(C("r15"), C("kr"), 15.0, A.is_equal)
+    vs(C("fm"), C("kr"), 15.0, A.is_lt)
+    vs(C("half"), C("fm"), -0.5, A.mult, 1.0, A.add)
+    for c0 in (0, 1024):
+        vs(("xb0", W0 + c0, W0 + c0 + 1024), ("xin", c0, c0 + 1024), C("half"), A.mult)
+    vs(mb, J, C("kg15"), A.is_equal)
+    vcopy(C("wf"), full("wti", 1))
+    vs(C("w1"), C("fm"), 1.0, A.add)
+    vs(C("wu"), C("wf"), C("w1"), A.mult)
+    vs(full("bu", 144), mb, C("wu"), A.mult)
+    vcopy(full("kmf", RO * M), full("kmi", RO * M))
+    vs(full("pwf"), full("ic"), C("kr"), A.add)
+    vcopy(PWP, full("pwf"))
+    vs(full("ib"), ij, C("k"), A.is_equal)
+    vs(C("f2"), C("fm"), 2.0, A.mult)
+    vs(full("lxa"), full("mb"), C("f2"), A.mult)
+    vs(full("lxc"), full("ib"), C("fm"), A.mult)
+    vt(full("lx"), full("lxa"), full("lxc"), A.add)
+    vs(C("flw"), C("fm"), 2.0, A.mult, -1.0, A.add)
+    vset(C("mone"), -1.0)
+    vs(C("dvc"), C("fm"), 40960.0, A.mult, -8192.0, A.add)
+    vs(C("dsc"), C("fm"), 16384.0, A.mult)
+    vs(C("bec"), C("fm"), 4096.0, A.mult)
+    for nm, cn in (("bf", "f2"), ("bs", "r15"), ("bdv", "dvc"), ("bds", "dsc"), ("be", "bec")):
+        vs(full(nm, 144), mb, C(cn), A.mult)
+    for nm, v in (("nib", -1.0), ("i16", 1.0), ("d2kb", 2048.0), ("dn8k", -8192.0), ("dvoid", 15728640.0), ("d2k16", 2048.0), ("ni16", -1.0), ("p2i", 2.0), ("m2i", -2.0)):
+        vs(full(nm), full("ib"), v, A.mult)
+    vcopy(full("pw16"), full("pwf"))
+    for m in range(1, 4):
+        vset(("cm", m * 128 - 128, m * 128), float(m))
+    vs(full("jb"), ij, 112, A.bitwise_and)
+    vcopy(C("kg"), C("ikg"))
+    vs(full("ob"), full("jb"), C("kg"), A.is_equal)
+    vs(full("mk16", 16), ("ij", 0, 16), C("kr"), A.is_equal)
+    vs(C("iodd"), C("ik"), 1, A.bitwise_and)
+    vcopy(C("odd"), C("iodd"))
+    vs(C("mk0"), C("kr"), 0.0, A.is_equal)
+    vs(C("padc"), C("kr"), 0.0, A.is_gt, float(TW), A.mult)
+    vt(C("padc"), C("padc"), C("kr"), A.add)
+    vs(C("dbl"), C("fm"), 1.0, A.add)
+    vset(("xb0", 0, W0), 0.0)
+    vset(("xb1", 0, W0), 0.0)
+    vset(full("msg"), 0)
+
+    last = 0
+    for k in range(4):
+        r = (k * 1024, k * 1024 + 1024)
+
+        def e(g, T, x, r=r):
+            for d, slot in x["own"]:
+                x["send"](d, ("tb%d" % slot,) + r, ("tmo",) + r, "ta%d" % slot, "lown")
+        last = add("g", 1.0, e, [("tmo",) + r], [], done=lambda x: ("lown", 0))
+    for k in range(RO):
+        add("x", 9.0 if k else 6.0, None, [], [("tb%d" % k, 0, TW)], done=(lambda x, k=k: ("ta%d" % k, x["ta"][k])), after=[last])
+        if k < RO - 1:
+            def e(g, T, x, k=k):
+                if x["fwd"][k] is not None:
+                    x["send"](x["fwd"][k], ("tb%d" % (k + 1), 0, TW), ("tb%d" % k, 0, TW), "ta%d" % (k + 1), "ls%d" % k)
+            last = add("g", 1.0, e, [("tb%d" % k, 0, TW)], [], done=(lambda x, k=k: ("ls%d" % k, x["lf"][k])))
+
+    wk = [0]
+
+    def work(n):
+        wk[0] += 1
+        return (("p3", "p4", "p7")[wk[0] % 3], 0, n)
+    msgops = {}
+    for t in range(RO):
+        xb, xn = "xb%d" % (t % 2), "xb%d" % (1 - t % 2)
+        X, XA = (xb, W0, W0 + P), (xb, 0, NX)
+
+        def pl(h, b=xb, o=W0):
+            return (b, o + 16 * PART[h][0], o + 16 * PART[h][1])
+        XC = ("xc", 0, 16 * N0)
+        add("d", 0.1, lambda g, T, x, s=pl(0), o=XC: g.sync.dma_start(_ap(T, o), _ap(T, s)), [pl(0)], [XC], done=(lambda x, t=t: ("xc%d" % t, 16)))
+        UP, FP = ("p0", 0, 128), ("p0", 128, 256)
+        mm(UP, wrapped("bu", xb, W0, P))
+        vcopy(full("ui"), UP)
+        vs(full("u"), full("ui"), 4095, A.bitwise_and)
+        vt(full("sq"), full("u"), full("u"), A.mult)
+        vs(full("sh"), full("sq"), 5, A.arith_shift_right)
+        for m in MORD:
+            c = (m * 128, m * 128 + 128)
+            vs(("p2",) + c, full("u"), ("kmf", t * M + m, t * M + m + 1), A.mult)
+            vt(("qv",) + c, full("sh"), ("p2",) + c, A.add)
+            vs(("qi",) + c, ("qv",) + c, 2047, A.bitwise_and)
+            vcopy(("ql",) + c, ("qi",) + c)
+        BST[0] = BX
+        for lo, hi in blocks(P):
+            w = work(512)
+            mm(w, [(full("lx"), (xb, W0 + lo, W0 + hi))])
+            sa(("xw", lo, hi), w, F.Identity, bias=C("r15"))
+        BST[0] = 0.0
+        mm(FP, wrapped("bf", xb, W0, P))
+        vs(full("f1"), FP, -1.0, A.add)
+        for m in MORD:
+            c = (m * 128, m * 128 + 128)
+            vcopy(("q16",) + c, ("qi",) + c)
+            vt(("eq",) + c, ("qi",) + c, PWP, A.is_equal)
+        for h in PORD:
+            h0, h1 = PART[h]
+            BST[0] = BP if h == PORD[0] else 0.0
+            for m in MORD:
+                wc = (m * 128 + h0, m * 128 + h1)
+                o = (m * P + 16 * h0, m * P + 16 * h1)
+                if (m, h) in VIT:
+                    vgt(("mx",) + o, full("xw", P), ("ql",) + wc, pl(h), A.max)
+                    parts = [(full("dn8k"), ("f1", h0, h1))] + wrapped("bdv", "mx", o[0], o[1] - o[0])
+                else:
+                    sg(("gm",) + o, X, ("ql",) + wc)
+                    for lo, hi in blocks(o[1] - o[0]):
+                        w = work(hi - lo)
+                        mm(w, [(full("ib"), ("gm", o[0] + lo, o[0] + hi)), (full("nib"), (xb, W0 + 16 * h0 + lo, W0 + 16 * h0 + hi))])
+                        sa(("ab", o[0] + lo, o[0] + hi), w, F.Abs)
+                    parts = wrapped("bds", "ab", o[0], o[1] - o[0])
+                parts = [(full("i16"), ("q16",) + wc), (full("dvoid"), ("eq",) + wc)] + parts
+                if m:
+                    parts.insert(0, (full("d2kb"), ("cm", m * 128 - 128, m * 128 - 128 + h1 - h0)))
+                mm(("p%d" % (1 + h), m * 128, m * 128 + h1 - h0), parts)
+        BST[0] = 0.0
+        tb = "tb%d" % t
+        TB = (tb, 0, TW)
+        for s in range(t):
+            i = _LK.index((t, s)) * 32
+            add("x", 3.0, None, [], [("land", i, i + 32)], done=(lambda x, s=s, t=t: ("m%d_%d" % (t, s), x["mn"][(t, s)])), after=[msgops[(t, s)]])
+            vcopy(full("upv", 16), ("land", i + 16, i + 32))
+            add("v", 0.15, lambda g, T, x, tb=tb, i=i: g.vector.tensor_copy(T[tb][:, 0:TW + 16].indirect(T.land[:, i:i + 1]), T.upv[:, 0:16]), [full("upv", 16), ("land", i, i + 32)], [(tb, 0, TW + 16)])
+        AT, E = ("p5", 256, 384), ("p6", 0, 128)
+        flips = 0
+        for h in PORD:
+            BST[0] = BP if h == PORD[0] else 0.0
+            c = PART[h]
+            n = c[1] - c[0]
+            pn = 16 * n
+            Zs = [("p%d" % (1 + h), m * 128, m * 128 + n) for m in range(4)]
+            US, SG = ("p5",) + c, ("p5", 128 + c[0], 128 + c[1])
+            vcopy(("b0",) + c, Zs[0])
+            vt(("b1",) + c, ("b0",) + c, Zs[2], A.min)
+            vt(("b2",) + c, ("b1",) + c, Zs[3 if (3, h) in VIT else 1], A.min)
+            vt(("bk",) + c, ("b2",) + c, Zs[1 if (3, h) in VIT else 3], A.min)
+            vs(("q",) + c, ("bk",) + c, 2047, A.bitwise_and)
+            vcopy(("qsl",) + c, ("q",) + c)
+            if h == 0:
+                vgt(full("sp", pn), X, ("qsl",) + c, XC, A.add)
+                mm(US, wrapped("bu", "sp", 0, pn))
+                vt(("uq",) + c, US, ("ui",) + c, A.subtract)
+            else:
+                sg(full("gq", pn), X, ("qsl",) + c)
+                mm(US, wrapped("bu", "gq", 0, pn))
+                vcopy(("uq",) + c, US)
+            vs(("uq2",) + c, ("uq",) + c, 4095, A.bitwise_and)
+            vt(("uu",) + c, ("uq2",) + c, ("u",) + c, A.mult)
+            vs(("h",) + c, ("uu",) + c, 4, A.arith_shift_right, 4095, A.bitwise_and)
+            vcopy(("hl",) + c, ("h",) + c)
+            vs(("di",) + c, ("bk",) + c, 13, A.arith_shift_right)
+            vcopy(("d16",) + c, ("di",) + c)
+            vs(("vc",) + c, ("di",) + c, 1919.0, A.is_ge, 2176.0, A.mult)
+            vcopy(("qs16",) + c, ("q",) + c)
+            o = 16 * c[0]
+            if h == 0:
+                vgt(full("rr", pn), TB, ("hl",) + c, full("sp", pn), A.subtract)
+                for lo, hi in blocks(pn):
+                    flips = sa(("ab2", o + lo, o + hi), ("rr", lo, hi), F.Abs)
+                mm(SG, wrapped("bs", "sp", 0, pn))
+            else:
+                sg(full("ga", pn), TB, ("hl",) + c)
+                for lo, hi in blocks(pn):
+                    w = work(hi - lo)
+                    mm(w, [(full("ib"), ("ga", lo, hi)), (full("nib"), ("gq", lo, hi)), (full("nib"), (xb, W0 + o + lo, W0 + o + hi))])
+                    flips = sa(("ab2", o + lo, o + hi), w, F.Abs)
+                mm(SG, wrapped("bs", "gq", 0, pn) + wrapped("bs", xb, W0 + o, pn))
+            mm(("p6",) + c, [(full("i16"), ("pw16",) + c), (full("d2k16"), ("d16",) + c), (full("d2kb"), ("vc",) + c)] + wrapped("be", "ab2", o, pn))
+        BST[0] = 0.0
+        sa(full("dir"), ("p5", 128, 256), F.Square, bias=C("mone"))
+        mm(AT, [(full("d2kb"), full("dir")), (full("i16"), full("qs16"))])
+        vt(full("cmn"), full("q"), PWP, A.min)
+        vt(full("cc"), full("cmn"), full("dir"), A.mult)
+        AFT.append(flips)
+        for lo, hi in blocks(P):
+            sa((xb, W0 + P + lo, W0 + P + hi), (xb, W0 + lo, W0 + hi), F.Identity, scale=C("flw"), bias=C("r15"))
+        AFT.clear()
+
+        def lowest(src, dst, kp):
+            vred(C("r1"), src, A.min)
+            vs(full("dg", 16), full("mk16", 16), C("r1"), A.mult)
+            mm(("p6", kp, kp + 16), [(full("ob"), full("dg", 16))])
+            vred(dst, ("p6", kp, kp + 16), A.min)
+
+        def fetch(oh, src, kmin, out):
+            vs(full(oh), src, kmin, A.is_equal)
+            vt(full("pr"), full(oh), AT, A.mult)
+            vred(C("ar"), full("pr"), A.add)
+            mm(out, [(full("ob"), C("ar"))])
+        A1, A2 = ("p6", 160, 161), ("p6", 224, 225)
+        lowest(E, C("kmin"), 128)
+        fetch("oh", E, C("kmin"), A1)
+        vcopy(("ka", 0, 1), C("kmin"))
+        vcopy(("ka", 1, 2), A1)
+        vs(full("pq", 2), full("ka", 2), 2047, A.bitwise_and)
+        vs(C("xC"), A1, 2048.0, A.is_lt, 4096.0, A.mult)
+        vs(C("dir"), A1, 2048.0, A.is_ge)
+        vt(C("a"), ("pq", 0, 1), ("pq", 1, 2), A.min)
+        vt(C("b"), ("pq", 0, 1), ("pq", 1, 2), A.max)
+        vs(C("aC"), C("a"), C("xC"), A.add)
+        BIG = float(2 ** 25)
+        vs(full("t1"), full("cc"), C("aC"), A.is_le, BIG, A.mult)
+        vs(full("t2"), full("cc"), C("b"), A.is_ge, BIG, A.mult)
+        vt(full("k2a"), full("t1"), E, A.max)
+        vt(full("k2"), full("k2a"), full("t2"), A.max)
+        vs(C("ba"), C("b"), C("a"), A.subtract)
+        vs(("nl", 0, 1), C("odd"), C("ba"), A.mult, C("a"), A.add)
+        sg(full("nc", 16), X, ("nl", 0, 1), bias=-0.125)
+        vs(C("nf"), ("nc", 1, 2), C("fm"), A.mult, ("nc", 0, 1), A.add)
+        vcopy(C("ni"), C("nf"))
+        vs((xb, 15, 16), C("ni"), C("half"), A.mult)
+        lin("xI", "dir", 4096.0, 0.0)
+        lin("inv", "dir", -1.0, 1.0)
+        lin("x3", "dir", -2048.0, 2048.0)
+        lin("an1", "a", -1.0, -1.0)
+        lin("xd", "b", -1.0, 2047.0)
+        lin("aI", "a", 1.0, C("xI"))
+        lin("bI", "b", 1.0, C("xI"))
+        lin("m1", "ba", 1.0, C("inv"))
+        lin("m3", "ba", C("dir"), C("x3"))
+        lin("K2", "ba", C("inv"), C("x3"))
+        lin("cdef", "ba", C("dir"), C("a"))
+        lin("ddef", "xd", C("dir"), C("b"))
+        pw = full("pw16")
+        G = [("gt", i * 128, i * 128 + 128) for i in range(7)]
+        vs(G[0], pw, C("a"), A.is_gt, C("m1"), A.mult)
+        vs(G[1], pw, C("aI"), A.subtract, 0.0, A.max)
+        vs(G[2], pw, C("bI"), A.subtract, 0.0, A.max)
+        vs(G[3], pw, C("a"), A.is_equal, C("an1"), A.mult)
+        PL = ("p1", 0, 128)
+        i16, n16 = full("i16"), full("ni16")
+        mm(PL, [(i16, pw), (i16, G[0]), (full("m2i"), G[1]), (full("p2i"), G[2]), (i16, G[3])], stop=False)
+        KK = full("k2")
+        lowest(KK, C("kmin2"), 192)
+        fetch("oh2", KK, C("kmin2"), A2)
+        vcopy(("kb", 0, 1), C("kmin2"))
+        vcopy(("kb", 1, 2), A2)
+        vs(full("pb", 2), full("kb", 2), 2047, A.bitwise_and)
+        vs(C("f"), C("kmin2"), float(2 ** 24), A.is_lt)
+        vt(C("c"), ("pb", 0, 1), ("pb", 1, 2), A.min)
+        vt(C("d"), ("pb", 0, 1), ("pb", 1, 2), A.max)
+        vs(C("valid"), C("d"), C("b"), A.is_gt, C("f"), A.mult)
+        vs(C("xc"), C("c"), C("cdef"), A.subtract)
+        vs(C("xe"), C("d"), C("ddef"), A.subtract)
+        vs(C("ce"), C("xc"), C("valid"), A.mult, C("cdef"), A.add)
+        vs(C("de"), C("xe"), C("valid"), A.mult, C("ddef"), A.add)
+        vs(C("t2"), C("de"), C("ba"), A.subtract)
+        vs(C("t3"), C("de"), C("ce"), A.subtract, C("a"), A.add)
+        vs(C("m2"), C("de"), C("ce"), A.subtract, C("K2"), A.subtract)
+        vs(C("m4"), C("de"), C("ce"), A.subtract, C("inv"), A.subtract)
+        vs(G[4], pw, C("t2"), A.is_gt, C("m2"), A.mult)
+        vs(G[5], pw, C("t3"), A.is_gt, C("m3"), A.mult)
+        vs(G[6], pw, C("de"), A.is_gt, C("m4"), A.mult)
+        mm(PL, [(n16, G[4]), (n16, G[5]), (i16, G[6])], start=False)
+        order = vs(full("pl"), PL, float(W0), A.add)
+        cut = 16 * NPV
+        if t < RO - 1:
+            vgs((xn, W0, W0 + cut), XA, ("pl", 0, NPV), 1.0)
+            sg((xn, W0 + cut, W0 + P), XA, ("pl", NPV, 128))
+            AFT.append(order)
+            vt(full("hpr"), full("oh"), full("h"), A.mult)
+            vred(C("har"), full("hpr"), A.add)
+            mm(("p6", 256, 257), [(full("ob"), C("har"))])
+            vcopy(C("hpf"), ("p6", 256, 257))
+            vs(("msg", t * 32, t * 32 + 1), C("hpf"), C("mk0"), A.mult, C("padc"), A.add)
+            vcopy(("msg", t * 32 + 16, t * 32 + 17), C("ni"))
+            for t2 in range(t + 1, RO):
+                def e(g, T, x, t=t, t2=t2):
+                    i = _LK.index((t2, t)) * 32
+                    x["send"](x["user"][t2], ("land", i, i + 32), ("msg", t * 32, t * 32 + 32), "m%d_%d" % (t2, t), "lmsg")
+                msgops[(t2, t)] = add("g", 1.0, e, [("msg", t * 32, t * 32 + 32)], [], done=lambda x: ("lmsg", 0))
+            AFT.clear()
+        else:
+            for h, (lo, hi) in enumerate(((0, cut), (cut, P))):
+                yo = ("yo", lo, hi)
+                if h:
+                    sg(yo, XA, ("pl", NPV, 128), scale=C("dbl"))
+                else:
+                    vgs(yo, XA, ("pl", 0, NPV), C("dbl"))
+                add("sd" if h else "d", 0.1, lambda g, T, x, h=h, yo=yo: (g.scalar if h else g.sync).dma_start(T.y[:, yo[1]:yo[2]], _ap(T, yo)), [yo], [], done=(lambda x, h=h: ("st%d" % h, 16)))
+    return ops
+
+
+_QS = {"v": "sv", "s": "ss", "t": "st", "g": "sg"}
+_CACHE = {}
+
+
+def plan():
+    if "o" in _CACHE:
+        return _CACHE["o"]
+    ops = build()
+    hist = {}
+    for i, o in enumerate(ops):
+        deps = set(o["after"])
+        q = o["qq"] = "s" if o["q"] == "sd" else o["q"]
+        rw = [(0, r) for r in o["reads"]] + [(1, r) for r in o["writes"]]
+        for kind, r in rw:
+            for (j, k2, a, b, q2) in hist.get(r[0], ()):
+                if (kind or k2) and a < r[2] and r[1] < b or _ps(r) and q2 != q:
+                    deps.add(j)
+        for kind, r in rw:
+            hl = hist.setdefault(r[0], [])
+            if kind:
+                hl[:] = [e for e in hl if not (r[1] <= e[2] and e[3] <= r[2] and (e[4] == q or not _ps(r)))]
+            hl.append((i, kind, r[1], r[2], q))
+        o["deps"] = sorted(deps)
+    n = len(ops)
+    succ = [[] for _ in ops]
+    for i, o in enumerate(ops):
+        for j in o["deps"]:
+            succ[j].append(i)
+    prio = [0.0] * n
+    for i in range(n - 1, -1, -1):
+        prio[i] = ops[i]["cost"] + ops[i]["boost"] + max([prio[j] + (SELF if ops[i]["qq"] == ops[j]["qq"] else WAKE) for j in succ[i]] + [0.0])
+    left = [len(o["deps"]) for o in ops]
+    est, fin, free, order = [0.0] * n, [0.0] * n, {}, []
+    ready = [i for i in range(n) if left[i] == 0]
+    while ready:
+        best, byq = None, {}
+        for i in ready:
+            byq.setdefault(ops[i]["qq"], []).append(i)
+        for q, lst in byq.items():
+            st = min(est[k] for k in lst)
+            if q != "x":
+                st = max(st, free.get(q, 0.0))
+            cand = sorted((k for k in lst if est[k] <= st + 1e-9), key=lambda k: (-prio[k], k))
+            pick = None
+            for i in cand:
+                if q == "x" or not any(prio[k] > prio[i] + 0.3 and st + ops[i]["cost"] - est[k] > est[k] - st for k in lst if st < est[k] < st + ops[i]["cost"]):
+                    pick = i
+                    break
+            if pick is None:
+                later = [k for k in lst if est[k] > st + 1e-9]
+                pick = min(later, key=lambda k: (est[k], -prio[k]))
+                st = est[pick]
+            if best is None or st < best[0]:
+                best = (st, pick, q)
+        st, i, q = best
+        ready.remove(i)
+        fin[i] = st + ops[i]["cost"]
+        if q != "x":
+            free[q] = fin[i] + 0.02
+        lat = 2.0 if ops[i]["q"] in ("d", "sd") else 0.0
+        order.append(i)
+        for j in succ[i]:
+            left[j] -= 1
+            est[j] = max(est[j], fin[i] + lat + (SELF if ops[j]["qq"] == q else WAKE))
+            if left[j] == 0:
+                ready.append(j)
+    cnt = {}
+    for i in order:
+        o = ops[i]
+        if o["done"] is None:
+            s = o["inc"] = _QS[o["q"]]
+            v = cnt[s] = cnt.get(s, 0) + 1
+            o["done"] = (lambda x, s=s, v=v: (s, v))
+    _CACHE["o"] = (ops, order, cnt, max(fin), fin)
+    return _CACHE["o"]
+
+
+def rank_program(g, core, T, topo):
+    rank = T.rank_of(core)
+    if rank is None:
+        return
+    ops, order, cnt, _, _ = plan()
+    N = len(T.cores)
+
+    def neng(a, b):
+        return len(topo.engines(T.cores[a % N], T.cores[b % N]))
+
+    def direct(r):
+        return topo.chip(T.cores[(r + RO) % N]) == topo.chip(T.cores[r % N])
+    tot = {}
+
+    def send(d, out, src, rsem, lsem):
+        dst = T.cores[d]
+        rid, pid, _ = topo.addr(dst)
+        g.remote_dma(_ap(T, out), _ap(T, src), T.sem[rsem], T.sem[lsem], pid, rid, topo.mask(core, dst))
+        tot[lsem] = tot.get(lsem, 0) + neng(rank, d)
+    dn, far = (rank - 1) % N, (rank - RO) % N
+    x = {"send": send, "user": {t: (rank - 1 - t) % N for t in range(RO)}}
+    x["own"] = [(dn, 0)] + ([(far, RO - 1)] if direct(far) else [])
+    x["fwd"] = [None if k == RO - 2 and direct(dn) else dn for k in range(RO - 1)]
+    x["lf"] = [0 if d is None else neng(rank, d) for d in x["fwd"]]
+    x["ta"] = [4 * neng(rank + 1, rank)] + [neng(rank + 1, rank)] * (RO - 1)
+    if direct(rank):
+        x["ta"][RO - 1] = 4 * neng(rank + RO, rank)
+    x["mn"] = {(t, s): neng(rank + 1 + t, rank) for (t, s) in _LK}
+    eng = {"v": g.vector, "s": g.scalar, "sd": g.scalar, "t": g.tensor, "g": g, "d": g.sync}
+    know, opk = {}, {}
+    for i in order:
+        o = ops[i]
+        q = o["qq"]
+        kn = dict(know.get(q, {})) if q != "x" else {}
+        if q == "x":
+            s, v = o["done"](x)
+            tot[s] = v
+        else:
+            need = {}
+            for j in o["deps"]:
+                s, v = ops[j]["done"](x)
+                if v > kn.get(s, 0) and v > need.get(s, (0, 0))[0]:
+                    need[s] = (v, j)
+            for s in list(need):
+                if any(s2 != s and opk[need[s2][1]].get(s, 0) >= need[s][0] for s2 in need):
+                    need.pop(s)
+            for s, (v, j) in need.items():
+                eng[o["q"]].wait_ge(T.sem[s], v)
+                for s2, v2 in list(opk[j].items()) + [(s, v)]:
+                    kn[s2] = max(kn.get(s2, 0), v2)
+            know[q] = kn
+            ins = o["emit"](g, T, x)
+            if o["q"] in ("d", "sd"):
+                s = o["done"](x)[0]
+                ins.then_inc(T.sem[s], 16)
+                tot[s] = 16
+            elif "inc" in o:
+                ins.then_inc(T.sem[o["inc"]], 1)
+        pre = dict(kn)
+        if "inc" in o:
+            s, v = o["done"](x)
+            pre[s] = max(pre.get(s, 0), v)
+        opk[i] = pre
+    for s, v in list(cnt.items()) + list(tot.items()):
+        if v > 0:
+            g.wait_ge(T.sem[s], v)

@@ -5,29 +5,29 @@ W0 = 16
 NX = W0 + 2 * P
 N0 = 56
 PART = ((0, N0), (N0, 128))
-VIT = {(0, 0), (0, 1), (1, 0), (1, 1), (3, 0)}
+VIT = {(0, 0), (0, 1), (1, 0), (1, 1), (3, 1)}
 PORD = (1, 0)
 MORD = (2, 0, 3, 1)
-NPV = 64
-BX, BP = 3.0, 1.0
+BX, BP, BQ, BU, BM, BE = 3.0, 1.0, 5.0, 6.0, -8.0, -2.0
 
 SCRATCH = {}
 _PS = ["p%d" % i for i in range(8)]
 _B2 = ("bfloat16", "float16", "uint16")
-_CS = {n: i for i, n in enumerate("kg15 kg kr k odd r15 fm half dbl flw wf wu w1 mk0 padc dvc dsc bec f2 mone r1 kmin ar har hpf nf kmin2 "
-                                  "a b dir inv ba aC aI bI m1 m3 x3 K2 cdef ddef xd an1 xC xI c d f valid xc xe ce de t2 t3 m2 m4".split())}
+_CS = {n: i for i, n in enumerate("kg15 kg kr k odd r15 fm half dbl flw wf wu w1 mk0 padc dvc dsc bec f2 mone r1 kmin har hpf nf kmin2 "
+                                  "a b dir inv ba aI bI m1 m3 x3 K2 cdef ddef xd an1 xC xI w f valid xc xe".split())}
 _CI = {n: i for i, n in enumerate("ik ikg ikr iodd ni".split())}
 for _a in _PS:
     SCRATCH[_a] = ("psum", [128, 512], "float32")
 for _d, _l in (("bfloat16", (("xin", P), ("tmo", TW), ("xb0", NX), ("xb1", NX), ("yo", P), ("xc", P), ("mb", 144), ("bu", 144), ("bf", 144), ("bs", 144), ("bds", 144), ("be", 144),
-                             ("ib", 128), ("nib", 128), ("d2kb", 128), ("dvoid", 128), ("lx", 128), ("cm", 384), ("eq", 512), ("gm", 4 * P), ("ab", 4 * P), ("vc", 128),
+                             ("ib", 128), ("nib", 128), ("d2kb", 128), ("dvoid", 128), ("dm4k", 128), ("lx", 128), ("cm", 384), ("eq", 512), ("gm", 4 * P), ("ab", 4 * P), ("vc", 128),
                              ("dir", 128), ("sp", P), ("gq", P), ("rr", P), ("ga", P), ("ab2", P), ("t1", 128), ("t2", 128)) + tuple(("tb%d" % k, TW + 16) for k in range(RO))),
                ("float16", (("bdv", 144), ("i16", 128), ("ni16", 128), ("p2i", 128), ("m2i", 128), ("d2k16", 128), ("dn8k", 128), ("pw16", 128), ("f1", 128), ("q16", 512),
-                            ("mx", 4 * P), ("d16", 128), ("qs16", 128), ("cc", 128), ("gt", 896))),
+                            ("mx", 4 * P), ("d16", 128), ("qs16", 128), ("cc", 128), ("cmn", 128), ("gt", 896))),
                ("float32", (("xw", P), ("cs", 64), ("kmf", RO * M), ("lxa", 128), ("lxc", 128), ("ob", 128), ("mk16", 16), ("pwf", 128), ("b0", 128), ("b1", 128), ("b2", 128),
-                            ("cmn", 128), ("dg", 16), ("oh", 128), ("pr", 128), ("hpr", 128), ("k2a", 128), ("k2", 128), ("oh2", 128), ("nc", 16), ("upv", 16))),
+                            ("aa", 4), ("pd", 5), ("qd", 5), ("qe", 3), ("dg", 16), ("oh", 128), ("pr", 256), ("hpr", 128), ("k2a", 128), ("k2", 128), ("oh2", 128), ("nc", 16),
+                            ("upv", 16))),
                ("int32", (("wti", 1), ("kmi", RO * M), ("ci", 8), ("ij", 144), ("ic", 128), ("jb", 128), ("ui", 128), ("u", 128), ("sq", 128), ("sh", 128), ("qv", 512), ("qi", 512),
-                          ("bk", 128), ("q", 128), ("di", 128), ("uq", 128), ("uq2", 128), ("uu", 128), ("h", 128), ("ka", 2), ("pq", 2), ("kb", 2), ("pb", 2))),
+                          ("bk", 128), ("q", 128), ("di", 128), ("uq", 128), ("uq2", 128), ("uu", 128), ("h", 128))),
                ("uint16", (("ql", 512), ("qsl", 128), ("hl", 128), ("nl", 2), ("pl", 128), ("msg", 128), ("land", 320)))):
     for _a, _c in _l:
         SCRATCH[_a] = ("sbuf", [128, _c], _d)
@@ -123,12 +123,16 @@ def build():
     def blocks(n):
         return [(b, min(b + 512, n)) for b in range(0, n, 512)]
 
+    TP = [(0, 256), (256, 1536), (1536, 2816), (2816, TW)]
+    BST[0] = 50.0
+    ld("lt0", "sd", ("tmo",) + TP[0], "tm", *TP[0])
+    ld("lw", "d", ("wti", 0, 1), "wt", 0, 1)
     ld("lx0", "d", ("xin", 0, 1024), "x", 0, 1024)
     ld("lx1", "sd", ("xin", 1024, P), "x", 1024, P)
-    ld("lw", "d", ("wti", 0, 1), "wt", 0, 1)
+    BST[0] = 0.0
     ld("lk", "d", ("kmi", 0, RO * M), "km", 0, RO * M)
-    for k in range(4):
-        ld("lt%d" % k, "d" if k % 2 else "sd", ("tmo", k * 1024, k * 1024 + 1024), "tm", k * 1024, k * 1024 + 1024)
+    for k in range(1, 4):
+        ld("lt%d" % k, "d" if k % 2 else "sd", ("tmo",) + TP[k], "tm", *TP[k])
 
     def iota(out, pat, base, cmul):
         add("g", 0.3, lambda g, T, x: g.iota(_ap(T, out), pat, base, cmul), [], [out])
@@ -169,7 +173,7 @@ def build():
     vs(C("bec"), C("fm"), 4096.0, A.mult)
     for nm, cn in (("bf", "f2"), ("bs", "r15"), ("bdv", "dvc"), ("bds", "dsc"), ("be", "bec")):
         vs(full(nm, 144), mb, C(cn), A.mult)
-    for nm, v in (("nib", -1.0), ("i16", 1.0), ("d2kb", 2048.0), ("dn8k", -8192.0), ("dvoid", 15728640.0), ("d2k16", 2048.0), ("ni16", -1.0), ("p2i", 2.0), ("m2i", -2.0)):
+    for nm, v in (("nib", -1.0), ("i16", 1.0), ("d2kb", 2048.0), ("dn8k", -8192.0), ("dvoid", 15728640.0), ("dm4k", -4096.0), ("d2k16", 2048.0), ("ni16", -1.0), ("p2i", 2.0), ("m2i", -2.0)):
         vs(full(nm), full("ib"), v, A.mult)
     vcopy(full("pw16"), full("pwf"))
     for m in range(1, 4):
@@ -190,19 +194,24 @@ def build():
 
     last = 0
     for k in range(4):
-        r = (k * 1024, k * 1024 + 1024)
+        r = TP[k]
+        last = add("g", 1.0, lambda g, T, x, r=r: x["send"](x["dn"], ("tb0",) + r, ("tmo",) + r, "ta0", "lown"), [("tmo",) + r], [], done=lambda x: ("lown", 0))
+    step = [last]
 
-        def e(g, T, x, r=r):
-            for d, slot in x["own"]:
-                x["send"](d, ("tb%d" % slot,) + r, ("tmo",) + r, "ta%d" % slot, "lown")
-        last = add("g", 1.0, e, [("tmo",) + r], [], done=lambda x: ("lown", 0))
-    for k in range(RO):
-        add("x", 9.0 if k else 6.0, None, [], [("tb%d" % k, 0, TW)], done=(lambda x, k=k: ("ta%d" % k, x["ta"][k])), after=[last])
+    def table(k, after):
+        add("x", 12.0 if k else 8.0, None, [], [("tb%d" % k, 0, TW)], done=(lambda x, k=k: ("ta%d" % k, x["ta"][k])), after=step[:1])
+
+        def far(g, T, x):
+            if x["far"] is not None:
+                x["send"](x["far"], ("tb%d" % (RO - 1), 0, TW), full("tmo", TW), "ta%d" % (RO - 1), "lown")
+
+        def e(g, T, x):
+            if x["fwd"][k] is not None:
+                x["send"](x["fwd"][k], ("tb%d" % (k + 1), 0, TW), ("tb%d" % k, 0, TW), "ta%d" % (k + 1), "ls%d" % k)
         if k < RO - 1:
-            def e(g, T, x, k=k):
-                if x["fwd"][k] is not None:
-                    x["send"](x["fwd"][k], ("tb%d" % (k + 1), 0, TW), ("tb%d" % k, 0, TW), "ta%d" % (k + 1), "ls%d" % k)
-            last = add("g", 1.0, e, [("tb%d" % k, 0, TW)], [], done=(lambda x, k=k: ("ls%d" % k, x["lf"][k])))
+            step[0] = add("g", 1.0, e, [("tb%d" % k, 0, TW)], [], done=(lambda x, k=k: ("ls%d" % k, x["lf"][k])), after=after)
+        if k == 1:
+            step.append(add("g", 1.0, far, [full("tmo", TW)], [], done=lambda x: ("lown", 0), after=[step[0]]))
 
     wk = [0]
 
@@ -216,10 +225,14 @@ def build():
 
         def pl(h, b=xb, o=W0):
             return (b, o + 16 * PART[h][0], o + 16 * PART[h][1])
+        table(t, [msgops[(s, t - 1)] for s in range(t, RO)] if t else [])
         XC = ("xc", 0, 16 * N0)
         add("d", 0.1, lambda g, T, x, s=pl(0), o=XC: g.sync.dma_start(_ap(T, o), _ap(T, s)), [pl(0)], [XC], done=(lambda x, t=t: ("xc%d" % t, 16)))
         UP, FP = ("p0", 0, 128), ("p0", 128, 256)
-        mm(UP, wrapped("bu", xb, W0, P))
+        BST[0] = BU
+        for h in range(2):
+            mm(("p0", 64 * h, 64 * h + 64), wrapped("bu", xb, W0 + 1024 * h, 1024))
+        BST[0] = 0.0
         vcopy(full("ui"), UP)
         vs(full("u"), full("ui"), 4095, A.bitwise_and)
         vt(full("sq"), full("u"), full("u"), A.mult)
@@ -235,7 +248,7 @@ def build():
             w = work(512)
             mm(w, [(full("lx"), (xb, W0 + lo, W0 + hi))])
             sa(("xw", lo, hi), w, F.Identity, bias=C("r15"))
-        BST[0] = 0.0
+        BST[0] = BQ
         mm(FP, wrapped("bf", xb, W0, P))
         vs(full("f1"), FP, -1.0, A.add)
         for m in MORD:
@@ -270,7 +283,7 @@ def build():
             add("x", 3.0, None, [], [("land", i, i + 32)], done=(lambda x, s=s, t=t: ("m%d_%d" % (t, s), x["mn"][(t, s)])), after=[msgops[(t, s)]])
             vcopy(full("upv", 16), ("land", i + 16, i + 32))
             add("v", 0.15, lambda g, T, x, tb=tb, i=i: g.vector.tensor_copy(T[tb][:, 0:TW + 16].indirect(T.land[:, i:i + 1]), T.upv[:, 0:16]), [full("upv", 16), ("land", i, i + 32)], [(tb, 0, TW + 16)])
-        AT, E = ("p5", 256, 384), ("p6", 0, 128)
+        SM, LG, E = ("p5", 256, 384), ("p5", 384, 512), ("p6", 0, 128)
         flips = 0
         for h in PORD:
             BST[0] = BP if h == PORD[0] else 0.0
@@ -302,10 +315,12 @@ def build():
             vs(("vc",) + c, ("di",) + c, 1919.0, A.is_ge, 2176.0, A.mult)
             vcopy(("qs16",) + c, ("q",) + c)
             o = 16 * c[0]
+            b0 = BST[0]
             if h == 0:
                 vgt(full("rr", pn), TB, ("hl",) + c, full("sp", pn), A.subtract)
                 for lo, hi in blocks(pn):
                     flips = sa(("ab2", o + lo, o + hi), ("rr", lo, hi), F.Abs)
+                BST[0] = b0 + BE
                 mm(SG, wrapped("bs", "sp", 0, pn))
             else:
                 sg(full("ga", pn), TB, ("hl",) + c)
@@ -313,13 +328,16 @@ def build():
                     w = work(hi - lo)
                     mm(w, [(full("ib"), ("ga", lo, hi)), (full("nib"), ("gq", lo, hi)), (full("nib"), (xb, W0 + o + lo, W0 + o + hi))])
                     flips = sa(("ab2", o + lo, o + hi), w, F.Abs)
+                BST[0] = b0 + BE
                 mm(SG, wrapped("bs", "gq", 0, pn) + wrapped("bs", xb, W0 + o, pn))
+            BST[0] = b0
             mm(("p6",) + c, [(full("i16"), ("pw16",) + c), (full("d2k16"), ("d16",) + c), (full("d2kb"), ("vc",) + c)] + wrapped("be", "ab2", o, pn))
         BST[0] = 0.0
         sa(full("dir"), ("p5", 128, 256), F.Square, bias=C("mone"))
-        mm(AT, [(full("d2kb"), full("dir")), (full("i16"), full("qs16"))])
         vt(full("cmn"), full("q"), PWP, A.min)
-        vt(full("cc"), full("cmn"), full("dir"), A.mult)
+        mm(LG, [(full("i16"), full("pw16")), (full("i16"), full("qs16")), (full("ni16"), full("cmn"))])
+        mm(SM, [(full("i16"), full("cmn")), (full("d2kb"), ("cm", 128, 256)), (full("dm4k"), full("dir"))])
+        vcopy(full("cc"), SM)
         AFT.append(flips)
         for lo, hi in blocks(P):
             sa((xb, W0 + P + lo, W0 + P + hi), (xb, W0 + lo, W0 + hi), F.Identity, scale=C("flw"), bias=C("r15"))
@@ -333,34 +351,32 @@ def build():
 
         def fetch(oh, src, kmin, out):
             vs(full(oh), src, kmin, A.is_equal)
-            vt(full("pr"), full(oh), AT, A.mult)
-            vred(C("ar"), full("pr"), A.add)
-            mm(out, [(full("ob"), C("ar"))])
-        A1, A2 = ("p6", 160, 161), ("p6", 224, 225)
+            for k, tile in ((0, SM), (1, LG)):
+                vt(("pr", 128 * k, 128 * k + 128), full(oh), tile, A.mult)
+                vred(("aa", k, k + 1), ("pr", 128 * k, 128 * k + 128), A.add)
+            mm(out, [(full("ob"), ("aa", 0, 2))])
+        A1, A2 = ("p6", 160, 162), ("p6", 224, 226)
+        aX, bX, cX, dX = ("p6", 160, 161), ("p6", 161, 162), ("p6", 224, 225), ("p6", 225, 226)
         lowest(E, C("kmin"), 128)
         fetch("oh", E, C("kmin"), A1)
-        vcopy(("ka", 0, 1), C("kmin"))
-        vcopy(("ka", 1, 2), A1)
-        vs(full("pq", 2), full("ka", 2), 2047, A.bitwise_and)
-        vs(C("xC"), A1, 2048.0, A.is_lt, 4096.0, A.mult)
-        vs(C("dir"), A1, 2048.0, A.is_ge)
-        vt(C("a"), ("pq", 0, 1), ("pq", 1, 2), A.min)
-        vt(C("b"), ("pq", 0, 1), ("pq", 1, 2), A.max)
-        vs(C("aC"), C("a"), C("xC"), A.add)
         BIG = float(2 ** 25)
-        vs(full("t1"), full("cc"), C("aC"), A.is_le, BIG, A.mult)
-        vs(full("t2"), full("cc"), C("b"), A.is_ge, BIG, A.mult)
+        vs(full("t1"), full("cc"), aX, A.is_le, BIG, A.mult)
+        vs(full("t2"), full("cc"), bX, A.is_ge, BIG, A.mult)
         vt(full("k2a"), full("t1"), E, A.max)
         vt(full("k2"), full("k2a"), full("t2"), A.max)
+        vs(C("inv"), aX, 4096.0, A.is_ge)
+        vs(C("xC"), aX, 4096.0, A.is_ge, -4096.0, A.mult)
+        vs(C("a"), aX, C("xC"), A.add)
+        vcopy(C("b"), bX)
         vs(C("ba"), C("b"), C("a"), A.subtract)
         vs(("nl", 0, 1), C("odd"), C("ba"), A.mult, C("a"), A.add)
         sg(full("nc", 16), X, ("nl", 0, 1), bias=-0.125)
         vs(C("nf"), ("nc", 1, 2), C("fm"), A.mult, ("nc", 0, 1), A.add)
         vcopy(C("ni"), C("nf"))
         vs((xb, 15, 16), C("ni"), C("half"), A.mult)
-        lin("xI", "dir", 4096.0, 0.0)
-        lin("inv", "dir", -1.0, 1.0)
-        lin("x3", "dir", -2048.0, 2048.0)
+        lin("dir", "inv", -1.0, 1.0)
+        lin("xI", "inv", -4096.0, 4096.0)
+        lin("x3", "inv", 2048.0, 0.0)
         lin("an1", "a", -1.0, -1.0)
         lin("xd", "b", -1.0, 2047.0)
         lin("aI", "a", 1.0, C("xI"))
@@ -370,6 +386,9 @@ def build():
         lin("K2", "ba", C("inv"), C("x3"))
         lin("cdef", "ba", C("dir"), C("a"))
         lin("ddef", "xd", C("dir"), C("b"))
+        lin("w", "cdef", -1.0, C("ddef"))
+        for k, (src, scale, bias) in enumerate((("ba", -1.0, "ddef"), ("ddef", 1.0, None), ("w", 1.0, "a"), ("K2", -1.0, "w"), ("inv", -1.0, "w"))):
+            sa(("pd", k, k + 1), C(src), F.Identity, scale=scale, bias=C(bias) if bias else 0.0)
         pw = full("pw16")
         G = [("gt", i * 128, i * 128 + 128) for i in range(7)]
         vs(G[0], pw, C("a"), A.is_gt, C("m1"), A.mult)
@@ -382,31 +401,26 @@ def build():
         KK = full("k2")
         lowest(KK, C("kmin2"), 192)
         fetch("oh2", KK, C("kmin2"), A2)
-        vcopy(("kb", 0, 1), C("kmin2"))
-        vcopy(("kb", 1, 2), A2)
-        vs(full("pb", 2), full("kb", 2), 2047, A.bitwise_and)
         vs(C("f"), C("kmin2"), float(2 ** 24), A.is_lt)
-        vt(C("c"), ("pb", 0, 1), ("pb", 1, 2), A.min)
-        vt(C("d"), ("pb", 0, 1), ("pb", 1, 2), A.max)
-        vs(C("valid"), C("d"), C("b"), A.is_gt, C("f"), A.mult)
-        vs(C("xc"), C("c"), C("cdef"), A.subtract)
-        vs(C("xe"), C("d"), C("ddef"), A.subtract)
-        vs(C("ce"), C("xc"), C("valid"), A.mult, C("cdef"), A.add)
-        vs(C("de"), C("xe"), C("valid"), A.mult, C("ddef"), A.add)
-        vs(C("t2"), C("de"), C("ba"), A.subtract)
-        vs(C("t3"), C("de"), C("ce"), A.subtract, C("a"), A.add)
-        vs(C("m2"), C("de"), C("ce"), A.subtract, C("K2"), A.subtract)
-        vs(C("m4"), C("de"), C("ce"), A.subtract, C("inv"), A.subtract)
-        vs(G[4], pw, C("t2"), A.is_gt, C("m2"), A.mult)
-        vs(G[5], pw, C("t3"), A.is_gt, C("m3"), A.mult)
-        vs(G[6], pw, C("de"), A.is_gt, C("m4"), A.mult)
+        vs(C("valid"), dX, C("b"), A.is_gt, C("f"), A.mult)
+        vs(C("xe"), dX, C("ddef"), A.subtract, C("valid"), A.mult)
+        vs(C("xc"), cX, C("cdef"), A.subtract, C("valid"), A.mult)
+        vs(full("qd", 5), full("pd", 5), C("xe"), A.add)
+        vs(full("qe", 3), ("qd", 2, 5), C("xc"), A.subtract)
+        vs(G[4], pw, ("qd", 0, 1), A.is_gt, ("qe", 1, 2), A.mult)
+        vs(G[5], pw, ("qe", 0, 1), A.is_gt, C("m3"), A.mult)
+        vs(G[6], pw, ("qd", 1, 2), A.is_gt, ("qe", 2, 3), A.mult)
         mm(PL, [(n16, G[4]), (n16, G[5]), (i16, G[6])], start=False)
         order = vs(full("pl"), PL, float(W0), A.add)
-        cut = 16 * NPV
         if t < RO - 1:
-            vgs((xn, W0, W0 + cut), XA, ("pl", 0, NPV), 1.0)
-            sg((xn, W0 + cut, W0 + P), XA, ("pl", NPV, 128))
+            for k in range(4):
+                o = (xn, W0 + 512 * k, W0 + 512 * k + 512)
+                if k % 2:
+                    sg(o, XA, ("pl", 32 * k, 32 * k + 32))
+                else:
+                    vgs(o, XA, ("pl", 32 * k, 32 * k + 32), 1.0)
             AFT.append(order)
+            BST[0] = BM
             vt(full("hpr"), full("oh"), full("h"), A.mult)
             vred(C("har"), full("hpr"), A.add)
             mm(("p6", 256, 257), [(full("ob"), C("har"))])
@@ -417,15 +431,16 @@ def build():
                 def e(g, T, x, t=t, t2=t2):
                     i = _LK.index((t2, t)) * 32
                     x["send"](x["user"][t2], ("land", i, i + 32), ("msg", t * 32, t * 32 + 32), "m%d_%d" % (t2, t), "lmsg")
-                msgops[(t2, t)] = add("g", 1.0, e, [("msg", t * 32, t * 32 + 32)], [], done=lambda x: ("lmsg", 0))
+                msgops[(t2, t)] = add("g", 1.0, e, [("msg", t * 32, t * 32 + 32)], [], done=lambda x: ("lmsg", 0), after=step)
             AFT.clear()
+            BST[0] = 0.0
         else:
-            for h, (lo, hi) in enumerate(((0, cut), (cut, P))):
-                yo = ("yo", lo, hi)
+            for h in range(2):
+                yo = ("yo", 1024 * h, 1024 * h + 1024)
                 if h:
-                    sg(yo, XA, ("pl", NPV, 128), scale=C("dbl"))
+                    sg(yo, XA, ("pl", 64, 128), scale=C("dbl"))
                 else:
-                    vgs(yo, XA, ("pl", 0, NPV), C("dbl"))
+                    vgs(yo, XA, ("pl", 0, 64), C("dbl"))
                 add("sd" if h else "d", 0.1, lambda g, T, x, h=h, yo=yo: (g.scalar if h else g.sync).dma_start(T.y[:, yo[1]:yo[2]], _ap(T, yo)), [yo], [], done=(lambda x, h=h: ("st%d" % h, 16)))
     return ops
 
@@ -440,7 +455,7 @@ def plan():
     ops = build()
     hist = {}
     for i, o in enumerate(ops):
-        deps = set(o["after"])
+        deps = set()
         q = o["qq"] = "s" if o["q"] == "sd" else o["q"]
         rw = [(0, r) for r in o["reads"]] + [(1, r) for r in o["writes"]]
         for kind, r in rw:
@@ -452,7 +467,8 @@ def plan():
             if kind:
                 hl[:] = [e for e in hl if not (r[1] <= e[2] and e[3] <= r[2] and (e[4] == q or not _ps(r)))]
             hl.append((i, kind, r[1], r[2], q))
-        o["deps"] = sorted(deps)
+        o["data"] = deps
+        o["deps"] = sorted(deps | set(o["after"]))
     n = len(ops)
     succ = [[] for _ in ops]
     for i, o in enumerate(ops):
@@ -528,12 +544,12 @@ def rank_program(g, core, T, topo):
         tot[lsem] = tot.get(lsem, 0) + neng(rank, d)
     dn, far = (rank - 1) % N, (rank - RO) % N
     x = {"send": send, "user": {t: (rank - 1 - t) % N for t in range(RO)}}
-    x["own"] = [(dn, 0)] + ([(far, RO - 1)] if direct(far) else [])
+    x["dn"], x["far"] = dn, far if direct(far) else None
     x["fwd"] = [None if k == RO - 2 and direct(dn) else dn for k in range(RO - 1)]
     x["lf"] = [0 if d is None else neng(rank, d) for d in x["fwd"]]
     x["ta"] = [4 * neng(rank + 1, rank)] + [neng(rank + 1, rank)] * (RO - 1)
     if direct(rank):
-        x["ta"][RO - 1] = 4 * neng(rank + RO, rank)
+        x["ta"][RO - 1] = neng(rank + RO, rank)
     x["mn"] = {(t, s): neng(rank + 1 + t, rank) for (t, s) in _LK}
     eng = {"v": g.vector, "s": g.scalar, "sd": g.scalar, "t": g.tensor, "g": g, "d": g.sync}
     know, opk = {}, {}
@@ -546,7 +562,7 @@ def rank_program(g, core, T, topo):
             tot[s] = v
         else:
             need = {}
-            for j in o["deps"]:
+            for j in sorted(o["data"]):
                 s, v = ops[j]["done"](x)
                 if v > kn.get(s, 0) and v > need.get(s, (0, 0))[0]:
                     need[s] = (v, j)

from concourse.mybir import AluOpType as A, AxisListType as AX, ActivationFunctionType as F

RO, M, P, TW = 5, 4, 2048, 4096
W0 = 16
NX = W0 + 2 * P
N0 = 56
PART = ((0, N0), (N0, 128))
VIT = {(0, 0), (0, 1), (1, 0), (1, 1), (3, 1)}
PORD = (1, 0)
MORD = (2, 0, 3, 1)
BX, BP, BQ, BU, BM, BE = 3.0, 1.0, 5.0, 6.0, -8.0, -2.0

SCRATCH = {}
_PS = ["p%d" % i for i in range(8)]
_B2 = ("bfloat16", "float16", "uint16")
_CS = {n: i for i, n in enumerate("kg15 kg kr k odd r15 fm half dbl flw wf wu w1 mk0 padc dvc dsc bec f2 mone r1 kmin har hpf nf kmin2 "
                                  "a b dir inv ba aI bI m1 m3 x3 K2 cdef ddef xd an1 xC xI w f valid xc xe".split())}
_CI = {n: i for i, n in enumerate("ik ikg ikr iodd ni".split())}
for _a in _PS:
    SCRATCH[_a] = ("psum", [128, 512], "float32")
for _d, _l in (("bfloat16", (("xin", P), ("tmo", TW), ("xb0", NX), ("xb1", NX), ("yo", P), ("xc", P), ("mb", 144), ("bu", 144), ("bf", 144), ("bs", 144), ("bds", 144), ("be", 144),
                             ("ib", 128), ("nib", 128), ("d2kb", 128), ("dvoid", 128), ("dm4k", 128), ("lx", 128), ("cm", 384), ("eq", 512), ("gm", 4 * P), ("ab", 4 * P), ("vc", 128),
                             ("dir", 128), ("sp", P), ("gq", P), ("rr", P), ("ga", P), ("ab2", P), ("t1", 128), ("t2", 128)) + tuple(("tb%d" % k, TW + 16) for k in range(RO))),
               ("float16", (("bdv", 144), ("i16", 128), ("ni16", 128), ("p2i", 128), ("m2i", 128), ("d2k16", 128), ("dn8k", 128), ("pw16", 128), ("f1", 128), ("q16", 512),
                            ("mx", 4 * P), ("d16", 128), ("qs16", 128), ("cc", 128), ("cmn", 128), ("gt", 896))),
               ("float32", (("xw", P), ("cs", 64), ("kmf", RO * M), ("lxa", 128), ("lxc", 128), ("ob", 128), ("mk16", 16), ("pwf", 128), ("b0", 128), ("b1", 128), ("b2", 128),
                            ("aa", 4), ("pd", 5), ("qd", 5), ("qe", 3), ("dg", 16), ("oh", 128), ("pr", 256), ("hpr", 128), ("k2a", 128), ("k2", 128), ("oh2", 128), ("nc", 16),
                            ("upv", 16))),
               ("int32", (("wti", 1), ("kmi", RO * M), ("ci", 8), ("ij", 144), ("ic", 128), ("jb", 128), ("ui", 128), ("u", 128), ("sq", 128), ("sh", 128), ("qv", 512), ("qi", 512),
                          ("bk", 128), ("q", 128), ("di", 128), ("uq", 128), ("uq2", 128), ("uu", 128), ("h", 128))),
               ("uint16", (("ql", 512), ("qsl", 128), ("hl", 128), ("nl", 2), ("pl", 128), ("msg", 128), ("land", 320)))):
    for _a, _c in _l:
        SCRATCH[_a] = ("sbuf", [128, _c], _d)
_LK = [(t, s) for t in range(1, RO) for s in range(t)]
SEMAPHORES = (["sv", "ss", "st", "sg", "lmsg", "lown", "lx0", "lx1", "lw", "lk", "lt0", "lt1", "lt2", "lt3", "st0", "st1"] + ["xc%d" % k for k in range(RO)]
              + ["ta%d" % k for k in range(RO)] + ["ls%d" % k for k in range(4)] + ["m%d_%d" % ts for ts in _LK])

CYC, TCY, GC, WAKE, SELF = 0.83e-3 * 1.25, 0.42e-3 * 1.25, 1.56, 0.15, 0.06


def _ap(T, r):
    return T[r[0]][:, r[1]:r[2]] if len(r) == 3 else T[r[0]][:, r[1]:r[2]:r[3]]


def _n(r):
    return r[2] - r[1]


def _ps(r):
    return r[0] in _PS


def C(n):
    return ("cs", _CS[n], _CS[n] + 1) if n in _CS else ("ci", _CI[n], _CI[n] + 1)


def build():
    ops, BST, AFT = [], [0.0], []

    def add(q, cost, emit, reads, writes, done=None, after=()):
        ops.append({"q": q, "cost": cost, "emit": emit, "reads": reads, "writes": writes, "done": done, "after": list(after) + AFT, "boost": BST[0]})
        return len(ops) - 1

    def isc(*xs):
        return [x for x in xs if isinstance(x, tuple)]

    def val(T, x):
        return _ap(T, x) if isinstance(x, tuple) else x

    def fast(*rs):
        return 0.5 if all((not _ps(r)) and SCRATCH[r[0]][2] in _B2 for r in rs) else 1.0

    def vt(out, a, b, op):
        c = _n(out) * (1 if _ps(a) or _ps(b) else 2)
        add("v", max(64, c) * CYC, lambda g, T, x: g.vector.tensor_tensor(_ap(T, out), _ap(T, a), _ap(T, b), op), [a, b], [out])

    def vs(out, a, s1, op0, s2=None, op1=None):
        def e(g, T, x):
            if op1 is None:
                return g.vector.tensor_scalar(_ap(T, out), _ap(T, a), val(T, s1), None, op0)
            return g.vector.tensor_scalar(_ap(T, out), _ap(T, a), val(T, s1), val(T, s2), op0, op1)
        return add("v", max(64, _n(out) * fast(out, a)) * CYC, e, [a] + isc(s1, s2), [out])

    def vcopy(out, a):
        add("v", max(64, _n(out) * fast(out, a)) * CYC, lambda g, T, x: g.vector.tensor_copy(_ap(T, out), _ap(T, a)), [a], [out])

    def vred(out, a, op):
        add("v", max(64, _n(a)) * CYC, lambda g, T, x: g.vector.tensor_reduce(_ap(T, out), _ap(T, a), AX.X, op), [a], [out])

    def vset(out, c):
        add("v", max(64, _n(out)) * CYC, lambda g, T, x: g.vector.memset(_ap(T, out), c), [], [out])

    def vgt(out, win, off, b, op):
        add("v", 0.05 + _n(out) * GC * CYC, lambda g, T, x: g.vector.tensor_tensor(_ap(T, out), _ap(T, win).indirect(_ap(T, off)), _ap(T, b), op), [win, off, b], [out])

    def vgs(out, win, off, s):
        add("v", 0.05 + _n(out) * GC * CYC, lambda g, T, x: g.vector.tensor_scalar(_ap(T, out), _ap(T, win).indirect(_ap(T, off)), val(T, s), None, A.mult), [win, off] + isc(s), [out])

    def sa(out, a, func, bias=0.0, scale=1.0):
        return add("s", (60 + max(64, _n(out))) * CYC, lambda g, T, x: g.scalar.activation(_ap(T, out), _ap(T, a), func, bias=val(T, bias), scale=val(T, scale)), [a] + isc(bias, scale), [out])

    def lin(out, a, scale, bias):
        sa(C(out), C(a), F.Identity, bias=bias, scale=scale)

    def sg(out, win, off, bias=0.0, scale=1.0):
        add("s", 0.065 + _n(out) * GC * CYC, lambda g, T, x: g.scalar.activation(_ap(T, out), _ap(T, win).indirect(_ap(T, off)), F.Identity, bias=bias, scale=val(T, scale)), [win, off] + isc(scale), [out])

    def mm(out, parts, start=True, stop=True):
        cost = len(parts) * max(64, _n(out)) * TCY * (4 if SCRATCH[parts[0][0][0]][2] == "float32" else 1)

        def e(g, T, x):
            for k, (l, r) in enumerate(parts):
                i = g.tensor.matmul(_ap(T, out), _ap(T, l), _ap(T, r), start and k == 0, stop and k == len(parts) - 1)
            return i
        add("t", cost, e, [y for lr in parts for y in lr] + ([] if start else [out]), [out])

    def wrapped(b, src, c0, n):
        return [((b, 15 - i, 143 - i), (src, c0 + i, c0 + n, 16)) for i in range(16)]

    def ld(sem, q, out, src, c0, c1):
        add(q, 0.1, lambda g, T, x: (g.sync if q == "d" else g.scalar).dma_start(_ap(T, out), T[src][:, c0:c1]), [], [out], done=lambda x: (sem, 16))

    def blocks(n):
        return [(b, min(b + 512, n)) for b in range(0, n, 512)]

    TP = [(0, 256), (256, 1536), (1536, 2816), (2816, TW)]
    BST[0] = 50.0
    ld("lt0", "sd", ("tmo",) + TP[0], "tm", *TP[0])
    ld("lw", "d", ("wti", 0, 1), "wt", 0, 1)
    ld("lx0", "d", ("xin", 0, 1024), "x", 0, 1024)
    ld("lx1", "sd", ("xin", 1024, P), "x", 1024, P)
    BST[0] = 0.0
    ld("lk", "d", ("kmi", 0, RO * M), "km", 0, RO * M)
    for k in range(1, 4):
        ld("lt%d" % k, "d" if k % 2 else "sd", ("tmo",) + TP[k], "tm", *TP[k])

    def iota(out, pat, base, cmul):
        add("g", 0.3, lambda g, T, x: g.iota(_ap(T, out), pat, base, cmul), [], [out])

    def full(n, c=128):
        return (n, 0, c)
    iota(C("ik"), [[1, 1]], 0, 1)
    iota(full("ij", 144), [[1, 144]], 0, 0)
    iota(full("ic"), [[16, 128]], 0, 0)
    ij, J, mb, PWP = full("ij"), full("ij", 144), full("mb", 144), ("p0", 256, 384)
    vs(C("ikg"), C("ik"), 112, A.bitwise_and)
    vs(C("ikr"), C("ik"), 15, A.bitwise_and)
    vcopy(C("k"), C("ik"))
    vcopy(C("kr"), C("ikr"))
    vs(C("kg15"), C("ikg"), 15.0, A.add)
    vs(C("r15"), C("kr"), 15.0, A.is_equal)
    vs(C("fm"), C("kr"), 15.0, A.is_lt)
    vs(C("half"), C("fm"), -0.5, A.mult, 1.0, A.add)
    for c0 in (0, 1024):
        vs(("xb0", W0 + c0, W0 + c0 + 1024), ("xin", c0, c0 + 1024), C("half"), A.mult)
    vs(mb, J, C("kg15"), A.is_equal)
    vcopy(C("wf"), full("wti", 1))
    vs(C("w1"), C("fm"), 1.0, A.add)
    vs(C("wu"), C("wf"), C("w1"), A.mult)
    vs(full("bu", 144), mb, C("wu"), A.mult)
    vcopy(full("kmf", RO * M), full("kmi", RO * M))
    vs(full("pwf"), full("ic"), C("kr"), A.add)
    vcopy(PWP, full("pwf"))
    vs(full("ib"), ij, C("k"), A.is_equal)
    vs(C("f2"), C("fm"), 2.0, A.mult)
    vs(full("lxa"), full("mb"), C("f2"), A.mult)
    vs(full("lxc"), full("ib"), C("fm"), A.mult)
    vt(full("lx"), full("lxa"), full("lxc"), A.add)
    vs(C("flw"), C("fm"), 2.0, A.mult, -1.0, A.add)
    vset(C("mone"), -1.0)
    vs(C("dvc"), C("fm"), 40960.0, A.mult, -8192.0, A.add)
    vs(C("dsc"), C("fm"), 16384.0, A.mult)
    vs(C("bec"), C("fm"), 4096.0, A.mult)
    for nm, cn in (("bf", "f2"), ("bs", "r15"), ("bdv", "dvc"), ("bds", "dsc"), ("be", "bec")):
        vs(full(nm, 144), mb, C(cn), A.mult)
    for nm, v in (("nib", -1.0), ("i16", 1.0), ("d2kb", 2048.0), ("dn8k", -8192.0), ("dvoid", 15728640.0), ("dm4k", -4096.0), ("d2k16", 2048.0), ("ni16", -1.0), ("p2i", 2.0), ("m2i", -2.0)):
        vs(full(nm), full("ib"), v, A.mult)
    vcopy(full("pw16"), full("pwf"))
    for m in range(1, 4):
        vset(("cm", m * 128 - 128, m * 128), float(m))
    vs(full("jb"), ij, 112, A.bitwise_and)
    vcopy(C("kg"), C("ikg"))
    vs(full("ob"), full("jb"), C("kg"), A.is_equal)
    vs(full("mk16", 16), ("ij", 0, 16), C("kr"), A.is_equal)
    vs(C("iodd"), C("ik"), 1, A.bitwise_and)
    vcopy(C("odd"), C("iodd"))
    vs(C("mk0"), C("kr"), 0.0, A.is_equal)
    vs(C("padc"), C("kr"), 0.0, A.is_gt, float(TW), A.mult)
    vt(C("padc"), C("padc"), C("kr"), A.add)
    vs(C("dbl"), C("fm"), 1.0, A.add)
    vset(("xb0", 0, W0), 0.0)
    vset(("xb1", 0, W0), 0.0)
    vset(full("msg"), 0)

    last = 0
    for k in range(4):
        r = TP[k]
        last = add("g", 1.0, lambda g, T, x, r=r: x["send"](x["dn"], ("tb0",) + r, ("tmo",) + r, "ta0", "lown"), [("tmo",) + r], [], done=lambda x: ("lown", 0))
    step = [last]

    def table(k, after):
        add("x", 12.0 if k else 8.0, None, [], [("tb%d" % k, 0, TW)], done=(lambda x, k=k: ("ta%d" % k, x["ta"][k])), after=step[:1])

        def far(g, T, x):
            if x["far"] is not None:
                x["send"](x["far"], ("tb%d" % (RO - 1), 0, TW), full("tmo", TW), "ta%d" % (RO - 1), "lown")

        def e(g, T, x):
            if x["fwd"][k] is not None:
                x["send"](x["fwd"][k], ("tb%d" % (k + 1), 0, TW), ("tb%d" % k, 0, TW), "ta%d" % (k + 1), "ls%d" % k)
        if k < RO - 1:
            step[0] = add("g", 1.0, e, [("tb%d" % k, 0, TW)], [], done=(lambda x, k=k: ("ls%d" % k, x["lf"][k])), after=after)
        if k == 1:
            step.append(add("g", 1.0, far, [full("tmo", TW)], [], done=lambda x: ("lown", 0), after=[step[0]]))

    wk = [0]

    def work(n):
        wk[0] += 1
        return (("p3", "p4", "p7")[wk[0] % 3], 0, n)
    msgops = {}
    for t in range(RO):
        xb, xn = "xb%d" % (t % 2), "xb%d" % (1 - t % 2)
        X, XA = (xb, W0, W0 + P), (xb, 0, NX)

        def pl(h, b=xb, o=W0):
            return (b, o + 16 * PART[h][0], o + 16 * PART[h][1])
        table(t, [msgops[(s, t - 1)] for s in range(t, RO)] if t else [])
        XC = ("xc", 0, 16 * N0)
        add("d", 0.1, lambda g, T, x, s=pl(0), o=XC: g.sync.dma_start(_ap(T, o), _ap(T, s)), [pl(0)], [XC], done=(lambda x, t=t: ("xc%d" % t, 16)))
        UP, FP = ("p0", 0, 128), ("p0", 128, 256)
        BST[0] = BU
        for h in range(2):
            mm(("p0", 64 * h, 64 * h + 64), wrapped("bu", xb, W0 + 1024 * h, 1024))
        BST[0] = 0.0
        vcopy(full("ui"), UP)
        vs(full("u"), full("ui"), 4095, A.bitwise_and)
        vt(full("sq"), full("u"), full("u"), A.mult)
        vs(full("sh"), full("sq"), 5, A.arith_shift_right)
        for m in MORD:
            c = (m * 128, m * 128 + 128)
            vs(("p2",) + c, full("u"), ("kmf", t * M + m, t * M + m + 1), A.mult)
            vt(("qv",) + c, full("sh"), ("p2",) + c, A.add)
            vs(("qi",) + c, ("qv",) + c, 2047, A.bitwise_and)
            vcopy(("ql",) + c, ("qi",) + c)
        BST[0] = BX
        for lo, hi in blocks(P):
            w = work(512)
            mm(w, [(full("lx"), (xb, W0 + lo, W0 + hi))])
            sa(("xw", lo, hi), w, F.Identity, bias=C("r15"))
        BST[0] = BQ
        mm(FP, wrapped("bf", xb, W0, P))
        vs(full("f1"), FP, -1.0, A.add)
        for m in MORD:
            c = (m * 128, m * 128 + 128)
            vcopy(("q16",) + c, ("qi",) + c)
            vt(("eq",) + c, ("qi",) + c, PWP, A.is_equal)
        for h in PORD:
            h0, h1 = PART[h]
            BST[0] = BP if h == PORD[0] else 0.0
            for m in MORD:
                wc = (m * 128 + h0, m * 128 + h1)
                o = (m * P + 16 * h0, m * P + 16 * h1)
                if (m, h) in VIT:
                    vgt(("mx",) + o, full("xw", P), ("ql",) + wc, pl(h), A.max)
                    parts = [(full("dn8k"), ("f1", h0, h1))] + wrapped("bdv", "mx", o[0], o[1] - o[0])
                else:
                    sg(("gm",) + o, X, ("ql",) + wc)
                    for lo, hi in blocks(o[1] - o[0]):
                        w = work(hi - lo)
                        mm(w, [(full("ib"), ("gm", o[0] + lo, o[0] + hi)), (full("nib"), (xb, W0 + 16 * h0 + lo, W0 + 16 * h0 + hi))])
                        sa(("ab", o[0] + lo, o[0] + hi), w, F.Abs)
                    parts = wrapped("bds", "ab", o[0], o[1] - o[0])
                parts = [(full("i16"), ("q16",) + wc), (full("dvoid"), ("eq",) + wc)] + parts
                if m:
                    parts.insert(0, (full("d2kb"), ("cm", m * 128 - 128, m * 128 - 128 + h1 - h0)))
                mm(("p%d" % (1 + h), m * 128, m * 128 + h1 - h0), parts)
        BST[0] = 0.0
        tb = "tb%d" % t
        TB = (tb, 0, TW)
        for s in range(t):
            i = _LK.index((t, s)) * 32
            add("x", 3.0, None, [], [("land", i, i + 32)], done=(lambda x, s=s, t=t: ("m%d_%d" % (t, s), x["mn"][(t, s)])), after=[msgops[(t, s)]])
            vcopy(full("upv", 16), ("land", i + 16, i + 32))
            add("v", 0.15, lambda g, T, x, tb=tb, i=i: g.vector.tensor_copy(T[tb][:, 0:TW + 16].indirect(T.land[:, i:i + 1]), T.upv[:, 0:16]), [full("upv", 16), ("land", i, i + 32)], [(tb, 0, TW + 16)])
        SM, LG, E = ("p5", 256, 384), ("p5", 384, 512), ("p6", 0, 128)
        flips = 0
        for h in PORD:
            BST[0] = BP if h == PORD[0] else 0.0
            c = PART[h]
            n = c[1] - c[0]
            pn = 16 * n
            Zs = [("p%d" % (1 + h), m * 128, m * 128 + n) for m in range(4)]
            US, SG = ("p5",) + c, ("p5", 128 + c[0], 128 + c[1])
            vcopy(("b0",) + c, Zs[0])
            vt(("b1",) + c, ("b0",) + c, Zs[2], A.min)
            vt(("b2",) + c, ("b1",) + c, Zs[3 if (3, h) in VIT else 1], A.min)
            vt(("bk",) + c, ("b2",) + c, Zs[1 if (3, h) in VIT else 3], A.min)
            vs(("q",) + c, ("bk",) + c, 2047, A.bitwise_and)
            vcopy(("qsl",) + c, ("q",) + c)
            if h == 0:
                vgt(full("sp", pn), X, ("qsl",) + c, XC, A.add)
                mm(US, wrapped("bu", "sp", 0, pn))
                vt(("uq",) + c, US, ("ui",) + c, A.subtract)
            else:
                sg(full("gq", pn), X, ("qsl",) + c)
                mm(US, wrapped("bu", "gq", 0, pn))
                vcopy(("uq",) + c, US)
            vs(("uq2",) + c, ("uq",) + c, 4095, A.bitwise_and)
            vt(("uu",) + c, ("uq2",) + c, ("u",) + c, A.mult)
            vs(("h",) + c, ("uu",) + c, 4, A.arith_shift_right, 4095, A.bitwise_and)
            vcopy(("hl",) + c, ("h",) + c)
            vs(("di",) + c, ("bk",) + c, 13, A.arith_shift_right)
            vcopy(("d16",) + c, ("di",) + c)
            vs(("vc",) + c, ("di",) + c, 1919.0, A.is_ge, 2176.0, A.mult)
            vcopy(("qs16",) + c, ("q",) + c)
            o = 16 * c[0]
            b0 = BST[0]
            if h == 0:
                vgt(full("rr", pn), TB, ("hl",) + c, full("sp", pn), A.subtract)
                for lo, hi in blocks(pn):
                    flips = sa(("ab2", o + lo, o + hi), ("rr", lo, hi), F.Abs)
                BST[0] = b0 + BE
                mm(SG, wrapped("bs", "sp", 0, pn))
            else:
                sg(full("ga", pn), TB, ("hl",) + c)
                for lo, hi in blocks(pn):
                    w = work(hi - lo)
                    mm(w, [(full("ib"), ("ga", lo, hi)), (full("nib"), ("gq", lo, hi)), (full("nib"), (xb, W0 + o + lo, W0 + o + hi))])
                    flips = sa(("ab2", o + lo, o + hi), w, F.Abs)
                BST[0] = b0 + BE
                mm(SG, wrapped("bs", "gq", 0, pn) + wrapped("bs", xb, W0 + o, pn))
            BST[0] = b0
            mm(("p6",) + c, [(full("i16"), ("pw16",) + c), (full("d2k16"), ("d16",) + c), (full("d2kb"), ("vc",) + c)] + wrapped("be", "ab2", o, pn))
        BST[0] = 0.0
        sa(full("dir"), ("p5", 128, 256), F.Square, bias=C("mone"))
        vt(full("cmn"), full("q"), PWP, A.min)
        mm(LG, [(full("i16"), full("pw16")), (full("i16"), full("qs16")), (full("ni16"), full("cmn"))])
        mm(SM, [(full("i16"), full("cmn")), (full("d2kb"), ("cm", 128, 256)), (full("dm4k"), full("dir"))])
        vcopy(full("cc"), SM)
        AFT.append(flips)
        for lo, hi in blocks(P):
            sa((xb, W0 + P + lo, W0 + P + hi), (xb, W0 + lo, W0 + hi), F.Identity, scale=C("flw"), bias=C("r15"))
        AFT.clear()

        def lowest(src, dst, kp):
            vred(C("r1"), src, A.min)
            vs(full("dg", 16), full("mk16", 16), C("r1"), A.mult)
            mm(("p6", kp, kp + 16), [(full("ob"), full("dg", 16))])
            vred(dst, ("p6", kp, kp + 16), A.min)

        def fetch(oh, src, kmin, out):
            vs(full(oh), src, kmin, A.is_equal)
            for k, tile in ((0, SM), (1, LG)):
                vt(("pr", 128 * k, 128 * k + 128), full(oh), tile, A.mult)
                vred(("aa", k, k + 1), ("pr", 128 * k, 128 * k + 128), A.add)
            mm(out, [(full("ob"), ("aa", 0, 2))])
        A1, A2 = ("p6", 160, 162), ("p6", 224, 226)
        aX, bX, cX, dX = ("p6", 160, 161), ("p6", 161, 162), ("p6", 224, 225), ("p6", 225, 226)
        lowest(E, C("kmin"), 128)
        fetch("oh", E, C("kmin"), A1)
        BIG = float(2 ** 25)
        vs(full("t1"), full("cc"), aX, A.is_le, BIG, A.mult)
        vs(full("t2"), full("cc"), bX, A.is_ge, BIG, A.mult)
        vt(full("k2a"), full("t1"), E, A.max)
        vt(full("k2"), full("k2a"), full("t2"), A.max)
        vs(C("inv"), aX, 4096.0, A.is_ge)
        vs(C("xC"), aX, 4096.0, A.is_ge, -4096.0, A.mult)
        vs(C("a"), aX, C("xC"), A.add)
        vcopy(C("b"), bX)
        vs(C("ba"), C("b"), C("a"), A.subtract)
        vs(("nl", 0, 1), C("odd"), C("ba"), A.mult, C("a"), A.add)
        sg(full("nc", 16), X, ("nl", 0, 1), bias=-0.125)
        vs(C("nf"), ("nc", 1, 2), C("fm"), A.mult, ("nc", 0, 1), A.add)
        vcopy(C("ni"), C("nf"))
        vs((xb, 15, 16), C("ni"), C("half"), A.mult)
        lin("dir", "inv", -1.0, 1.0)
        lin("xI", "inv", -4096.0, 4096.0)
        lin("x3", "inv", 2048.0, 0.0)
        lin("an1", "a", -1.0, -1.0)
        lin("xd", "b", -1.0, 2047.0)
        lin("aI", "a", 1.0, C("xI"))
        lin("bI", "b", 1.0, C("xI"))
        lin("m1", "ba", 1.0, C("inv"))
        lin("m3", "ba", C("dir"), C("x3"))
        lin("K2", "ba", C("inv"), C("x3"))
        lin("cdef", "ba", C("dir"), C("a"))
        lin("ddef", "xd", C("dir"), C("b"))
        lin("w", "cdef", -1.0, C("ddef"))
        for k, (src, scale, bias) in enumerate((("ba", -1.0, "ddef"), ("ddef", 1.0, None), ("w", 1.0, "a"), ("K2", -1.0, "w"), ("inv", -1.0, "w"))):
            sa(("pd", k, k + 1), C(src), F.Identity, scale=scale, bias=C(bias) if bias else 0.0)
        pw = full("pw16")
        G = [("gt", i * 128, i * 128 + 128) for i in range(7)]
        vs(G[0], pw, C("a"), A.is_gt, C("m1"), A.mult)
        vs(G[1], pw, C("aI"), A.subtract, 0.0, A.max)
        vs(G[2], pw, C("bI"), A.subtract, 0.0, A.max)
        vs(G[3], pw, C("a"), A.is_equal, C("an1"), A.mult)
        PL = ("p1", 0, 128)
        i16, n16 = full("i16"), full("ni16")
        mm(PL, [(i16, pw), (i16, G[0]), (full("m2i"), G[1]), (full("p2i"), G[2]), (i16, G[3])], stop=False)
        KK = full("k2")
        lowest(KK, C("kmin2"), 192)
        fetch("oh2", KK, C("kmin2"), A2)
        vs(C("f"), C("kmin2"), float(2 ** 24), A.is_lt)
        vs(C("valid"), dX, C("b"), A.is_gt, C("f"), A.mult)
        vs(C("xe"), dX, C("ddef"), A.subtract, C("valid"), A.mult)
        vs(C("xc"), cX, C("cdef"), A.subtract, C("valid"), A.mult)
        vs(full("qd", 5), full("pd", 5), C("xe"), A.add)
        vs(full("qe", 3), ("qd", 2, 5), C("xc"), A.subtract)
        vs(G[4], pw, ("qd", 0, 1), A.is_gt, ("qe", 1, 2), A.mult)
        vs(G[5], pw, ("qe", 0, 1), A.is_gt, C("m3"), A.mult)
        vs(G[6], pw, ("qd", 1, 2), A.is_gt, ("qe", 2, 3), A.mult)
        mm(PL, [(n16, G[4]), (n16, G[5]), (i16, G[6])], start=False)
        order = vs(full("pl"), PL, float(W0), A.add)
        if t < RO - 1:
            for k in range(4):
                o = (xn, W0 + 512 * k, W0 + 512 * k + 512)
                if k % 2:
                    sg(o, XA, ("pl", 32 * k, 32 * k + 32))
                else:
                    vgs(o, XA, ("pl", 32 * k, 32 * k + 32), 1.0)
            AFT.append(order)
            BST[0] = BM
            vt(full("hpr"), full("oh"), full("h"), A.mult)
            vred(C("har"), full("hpr"), A.add)
            mm(("p6", 256, 257), [(full("ob"), C("har"))])
            vcopy(C("hpf"), ("p6", 256, 257))
            vs(("msg", t * 32, t * 32 + 1), C("hpf"), C("mk0"), A.mult, C("padc"), A.add)
            vcopy(("msg", t * 32 + 16, t * 32 + 17), C("ni"))
            for t2 in range(t + 1, RO):
                def e(g, T, x, t=t, t2=t2):
                    i = _LK.index((t2, t)) * 32
                    x["send"](x["user"][t2], ("land", i, i + 32), ("msg", t * 32, t * 32 + 32), "m%d_%d" % (t2, t), "lmsg")
                msgops[(t2, t)] = add("g", 1.0, e, [("msg", t * 32, t * 32 + 32)], [], done=lambda x: ("lmsg", 0), after=step)
            AFT.clear()
            BST[0] = 0.0
        else:
            for h in range(2):
                yo = ("yo", 1024 * h, 1024 * h + 1024)
                if h:
                    sg(yo, XA, ("pl", 64, 128), scale=C("dbl"))
                else:
                    vgs(yo, XA, ("pl", 0, 64), C("dbl"))
                add("sd" if h else "d", 0.1, lambda g, T, x, h=h, yo=yo: (g.scalar if h else g.sync).dma_start(T.y[:, yo[1]:yo[2]], _ap(T, yo)), [yo], [], done=(lambda x, h=h: ("st%d" % h, 16)))
    return ops


_QS = {"v": "sv", "s": "ss", "t": "st", "g": "sg"}
_CACHE = {}


def plan():
    if "o" in _CACHE:
        return _CACHE["o"]
    ops = build()
    hist = {}
    for i, o in enumerate(ops):
        deps = set()
        q = o["qq"] = "s" if o["q"] == "sd" else o["q"]
        rw = [(0, r) for r in o["reads"]] + [(1, r) for r in o["writes"]]
        for kind, r in rw:
            for (j, k2, a, b, q2) in hist.get(r[0], ()):
                if (kind or k2) and a < r[2] and r[1] < b or _ps(r) and q2 != q:
                    deps.add(j)
        for kind, r in rw:
            hl = hist.setdefault(r[0], [])
            if kind:
                hl[:] = [e for e in hl if not (r[1] <= e[2] and e[3] <= r[2] and (e[4] == q or not _ps(r)))]
            hl.append((i, kind, r[1], r[2], q))
        o["data"] = deps
        o["deps"] = sorted(deps | set(o["after"]))
    n = len(ops)
    succ = [[] for _ in ops]
    for i, o in enumerate(ops):
        for j in o["deps"]:
            succ[j].append(i)
    prio = [0.0] * n
    for i in range(n - 1, -1, -1):
        prio[i] = ops[i]["cost"] + ops[i]["boost"] + max([prio[j] + (SELF if ops[i]["qq"] == ops[j]["qq"] else WAKE) for j in succ[i]] + [0.0])
    left = [len(o["deps"]) for o in ops]
    est, fin, free, order = [0.0] * n, [0.0] * n, {}, []
    ready = [i for i in range(n) if left[i] == 0]
    while ready:
        best, byq = None, {}
        for i in ready:
            byq.setdefault(ops[i]["qq"], []).append(i)
        for q, lst in byq.items():
            st = min(est[k] for k in lst)
            if q != "x":
                st = max(st, free.get(q, 0.0))
            cand = sorted((k for k in lst if est[k] <= st + 1e-9), key=lambda k: (-prio[k], k))
            pick = None
            for i in cand:
                if q == "x" or not any(prio[k] > prio[i] + 0.3 and st + ops[i]["cost"] - est[k] > est[k] - st for k in lst if st < est[k] < st + ops[i]["cost"]):
                    pick = i
                    break
            if pick is None:
                later = [k for k in lst if est[k] > st + 1e-9]
                pick = min(later, key=lambda k: (est[k], -prio[k]))
                st = est[pick]
            if best is None or st < best[0]:
                best = (st, pick, q)
        st, i, q = best
        ready.remove(i)
        fin[i] = st + ops[i]["cost"]
        if q != "x":
            free[q] = fin[i] + 0.02
        lat = 2.0 if ops[i]["q"] in ("d", "sd") else 0.0
        order.append(i)
        for j in succ[i]:
            left[j] -= 1
            est[j] = max(est[j], fin[i] + lat + (SELF if ops[j]["qq"] == q else WAKE))
            if left[j] == 0:
                ready.append(j)
    cnt = {}
    for i in order:
        o = ops[i]
        if o["done"] is None:
            s = o["inc"] = _QS[o["q"]]
            v = cnt[s] = cnt.get(s, 0) + 1
            o["done"] = (lambda x, s=s, v=v: (s, v))
    _CACHE["o"] = (ops, order, cnt, max(fin), fin)
    return _CACHE["o"]


def rank_program(g, core, T, topo):
    rank = T.rank_of(core)
    if rank is None:
        return
    ops, order, cnt, _, _ = plan()
    N = len(T.cores)

    def neng(a, b):
        return len(topo.engines(T.cores[a % N], T.cores[b % N]))

    def direct(r):
        return topo.chip(T.cores[(r + RO) % N]) == topo.chip(T.cores[r % N])
    tot = {}

    def send(d, out, src, rsem, lsem):
        dst = T.cores[d]
        rid, pid, _ = topo.addr(dst)
        g.remote_dma(_ap(T, out), _ap(T, src), T.sem[rsem], T.sem[lsem], pid, rid, topo.mask(core, dst))
        tot[lsem] = tot.get(lsem, 0) + neng(rank, d)
    dn, far = (rank - 1) % N, (rank - RO) % N
    x = {"send": send, "user": {t: (rank - 1 - t) % N for t in range(RO)}}
    x["dn"], x["far"] = dn, far if direct(far) else None
    x["fwd"] = [None if k == RO - 2 and direct(dn) else dn for k in range(RO - 1)]
    x["lf"] = [0 if d is None else neng(rank, d) for d in x["fwd"]]
    x["ta"] = [4 * neng(rank + 1, rank)] + [neng(rank + 1, rank)] * (RO - 1)
    if direct(rank):
        x["ta"][RO - 1] = neng(rank + RO, rank)
    x["mn"] = {(t, s): neng(rank + 1 + t, rank) for (t, s) in _LK}
    eng = {"v": g.vector, "s": g.scalar, "sd": g.scalar, "t": g.tensor, "g": g, "d": g.sync}
    know, opk = {}, {}
    for i in order:
        o = ops[i]
        q = o["qq"]
        kn = dict(know.get(q, {})) if q != "x" else {}
        if q == "x":
            s, v = o["done"](x)
            tot[s] = v
        else:
            need = {}
            for j in sorted(o["data"]):
                s, v = ops[j]["done"](x)
                if v > kn.get(s, 0) and v > need.get(s, (0, 0))[0]:
                    need[s] = (v, j)
            for s in list(need):
                if any(s2 != s and opk[need[s2][1]].get(s, 0) >= need[s][0] for s2 in need):
                    need.pop(s)
            for s, (v, j) in need.items():
                eng[o["q"]].wait_ge(T.sem[s], v)
                for s2, v2 in list(opk[j].items()) + [(s, v)]:
                    kn[s2] = max(kn.get(s2, 0), v2)
            know[q] = kn
            ins = o["emit"](g, T, x)
            if o["q"] in ("d", "sd"):
                s = o["done"](x)[0]
                ins.then_inc(T.sem[s], 16)
                tot[s] = 16
            elif "inc" in o:
                ins.then_inc(T.sem[o["inc"]], 1)
        pre = dict(kn)
        if "inc" in o:
            s, v = o["done"](x)
            pre[s] = max(pre.get(s, 0), v)
        opk[i] = pre
    for s, v in list(cnt.items()) + list(tot.items()):
        if v > 0:
            g.wait_ge(T.sem[s], v)
